import numpy as np, ml_dtypes
CORES = [3,5,19,21,35,37,51,53,67,69]
N = 10
T, KB = 2048, 2048
CAPP = 512
def entries(a): return a.T.reshape(-1)
def pack(v, P): return np.ascontiguousarray(np.asarray(v, np.int32).reshape(-1, P).T)
def order(K):
    return np.argsort(K, kind="stable")
def most(K):
    o = order(K); return int(np.bincount(o // T * N + np.arange(N * T) // T, minlength=N * N).max())
def lists(rng, how):
    i, G = np.arange(N), T // CAPP
    if how == "uniform":
        for again in range(50):
            K = rng.integers(0, KB, (N, T))
            if most(K.reshape(-1)) <= CAPP: break
        else: K = np.broadcast_to(np.arange(T) % KB, (N, T)).copy()
    else:
        if how == "uneven":
            t = rng.integers(0, CAPP + 1, N)
            if t.sum() < T: t = CAPP - t
            t[0] = CAPP; w = np.diff(np.minimum(np.cumsum(t), T), prepend=0); L = w[(rng.permutation(N)[:, None] - rng.permutation(N)) % N]
        else:
            w = np.zeros(N, int); w[(G * (ord(how[-1]) - 97) + np.arange(G)) % N] = CAPP; L = w[(i[:, None] - i) % N]
        a = N - 1 - np.argmax(L[::-1] > 0, axis=0)
        m = np.minimum(rng.integers(1, CAPP, N - 1), L[a[:-1], i[1:]])
        v = np.nonzero((L[a[:-1], i[:-1]] == CAPP) & (L[a[:-1], i[1:]] == CAPP) & (a[:-1] != np.append(-1, a[:-2])))[0]
        if len(v): m[rng.choice(v)] = CAPP
        C = L.copy(); C[a[:-1], i[:-1]] += m; C[a[:-1], i[1:]] -= m
        kv = np.sort(rng.permutation(KB)[:N]); K = np.stack([rng.permutation(np.repeat(kv, c)) for c in C]); K[::3] = np.sort(K[::3], axis=1)
    return {"key": np.stack([pack(k, 16) for k in K])}
def setup_inputs(rng):
    return dict({"x": rng.standard_normal((N, 128, T), dtype=np.float32).astype(ml_dtypes.bfloat16)}, **lists(rng, "uniform"))
def setup_inputs_fulla(rng):
    d = setup_inputs(rng); d.update(lists(rng, "fulla"))
    for k in ("x",): d[k] = (d[k].astype(np.float32) * 1048576.0).astype(d[k].dtype)
    return d
def setup_inputs_fullb(rng):
    d = setup_inputs(rng); d.update(lists(rng, "fullb"))
    for k in ("x",): d[k] = (d[k].astype(np.float32) * (1 / 1024.0)).astype(d[k].dtype)
    return d
def setup_inputs_fullc(rng):
    d = setup_inputs(rng); d.update(lists(rng, "fullc"))
    return d
def setup_inputs_uneven(rng):
    d = setup_inputs(rng); d.update(lists(rng, "uneven"))
    return d
def check_inputs(x):
    bad = []
    if x["key"].min() < 0 or x["key"].max() >= KB: bad.append("key out of range")
    if most(np.concatenate([entries(a) for a in x["key"]])) > CAPP: bad.append("more than CAPP columns go from one rank to one rank")
    return bad
def reference(x, key):
    X = np.concatenate(list(x), axis=1); K = np.concatenate([entries(a) for a in key])
    Y = X[:, order(K)]
    return {"y": np.stack([Y[:, T * r:T * r + T] for r in range(N)])}

@@ -1,0 +1,354 @@
+from concourse.bass import DstId, RemoteDMATransfer
+from concourse.mybir import AluOpType as Op, AxisListType, ActivationFunctionType as Act
+
+B16, F16, F32, I32, U16 = "bfloat16", "float16", "float32", "int32", "uint16"
+N, NT, CAP = 10, 2048, 512
+XS, NS, NMAP = 1664, 7, 6
+SCRATCH = {
+    "idf": ("sbuf", [16, 16], F32), "rowsel": ("sbuf", [16, 2048], F16), "z16": ("sbuf", [16, 240], F16),
+    "key16": ("sbuf", [16, 128], I32), "kint": ("sbuf", [16, 256], I32), "kd": ("sbuf", [16, 384], F16),
+    "ktt": ("sbuf", [16, 128], F16),
+    "sl": ("sbuf", [128, 2048], F16), "sr": ("sbuf", [128, 2048], F16), "slist": ("sbuf", [128, 128], U16),
+    "ml": ("sbuf", [128, 2048], F16), "mr": ("sbuf", [128, 2560], F16), "mt": ("sbuf", [128, 10, 32], F16),
+    "hs": ("sbuf", [128, 16], F16), "hl": ("sbuf", [128, 160], F16), "lm": ("sbuf", [128, 320], F16),
+    "wl": ("sbuf", [128, 320], U16), "flist": ("sbuf", [128, 128], U16),
+    "xb": ("sbuf", [128, 2048], B16), "xs": ("sbuf", [128, 2048], B16),
+    "wnd": ("sbuf", [128, 5120], B16), "ld": ("sbuf", [128, 5120], B16), "yb": ("sbuf", [128, 2048], B16),
+}
+for _k in ("pk", "ph", "pt", "pl", "kb0", "kb1", "kb2", "kb3"):
+    SCRATCH[_k] = ("psum", [128, 512], F32)
+PARTS = {
+    ("ff", F32): [("pcol", 1), ("p112", 1), ("pdig", 2), ("io32", 32), ("jv", 16), ("abias", 1), ("m8", 8), ("lst", 128),
+                  ("ktd", 48), ("scan0", 257), ("rowt", 2), ("prod", 256), ("scan", 256), ("lr", 16), ("divf", 16),
+                  ("dmul", 16), ("modf", 16), ("base", 160), ("xr", 160), ("scb", 160), ("dt", 16), ("prod2", 256),
+                  ("scan2", 256), ("pos", 16), ("lr1", 16), ("pdivf", 16), ("pmul", 16), ("pmod", 16)],
+    ("ii", I32): [("pint", 1), ("pbit", 2), ("divi", 16), ("pdivi", 16)],
+    ("hh", F16): [("ident", 128), ("pen", 512), ("onesf", 128), ("rl", 1024), ("wrap", 128), ("kabs", 2048), ("oht", 2048),
+                  ("tbl", 256), ("hp", 176), ("junk", 160), ("hrep", 160), ("xm", 160), ("dh", 16), ("dl", 16),
+                  ("t1", 160), ("t2", 64), ("t3", 32), ("t4", 32)],
+    ("bb", B16): [("iow", 258), ("io16", 256), ("ones", 258), ("segm", 256), ("fabs", 256), ("oha", 2048), ("ohf", 256),
+                  ("eq", 2048)],
+}
+ALIAS = {}
+for (_b, _d), _l in PARTS.items():
+    _o = 0
+    for _n, _w in _l:
+        ALIAS[_n] = (_b, _o, _w)
+        _o += _w
+    SCRATCH[_b] = ("sbuf", [128, _o], _d)
+SEMAPHORES = ["V", "S", "T", "G", "key", "x", "st", "hist", "map", "dat", "loc"]
+
+
+def rank_program(g, core, T, topo):
+    r = T.rank_of(core)
+    if r is None:
+        return
+    eng = {"V": g.vector, "S": g.scalar, "T": g.tensor, "G": g, "Y": g.sync}
+    log, seen, cnt = {}, {}, {}
+
+    def A(name, lo=0, hi=None, step=1, p=None):
+        buf, off, w = ALIAS[name] if name in ALIAS else (name, 0, T[name].shape[1])
+        t = T[buf]
+        lo, hi = off + lo, off + (w if hi is None else hi)
+        p = t.shape[0] if p is None else p
+        return (t[0:p, lo:hi:step] if step > 1 else t[0:p, lo:hi]), buf, lo, hi
+
+    def guard(q, outs, ins):
+        want = {}
+        for w, accs in ((True, outs), (False, ins)):
+            for _, name, lo, hi in accs:
+                bank = SCRATCH[name][0] == "psum"
+                for sem, c, e, iw, l, h in log.get(name, []):
+                    meet = l < hi and lo < h
+                    if e == q:
+                        hit = meet and iw and not w
+                    else:
+                        hit = bank or (meet and (iw or w))
+                    if hit:
+                        want[sem] = max(want.get(sem, 0), c)
+        for sem, c in want.items():
+            if seen.get((q, sem), 0) < c:
+                eng[q].wait_ge(T.sem[sem], c)
+                seen[(q, sem)] = c
+
+    def note(sem, c, e, outs, ins):
+        for w, accs in ((True, outs), (False, ins)):
+            for _, name, lo, hi in accs:
+                log.setdefault(name, []).append((sem, c, e, w, lo, hi))
+
+    def do(q, fn, outs, ins):
+        guard(q, outs, ins)
+        cnt[q] = cnt.get(q, 0) + 1
+        fn().then_inc(T.sem[q], 1)
+        note(q, cnt[q], q, outs, ins)
+
+    def ts(o, i, s1, op0, s2=None, op1=None):
+        sc = [s for s in (s1, s2) if isinstance(s, tuple)]
+        a1 = s1[0] if isinstance(s1, tuple) else s1
+        a2 = s2[0] if isinstance(s2, tuple) else s2
+        if op1 is None:
+            do("V", lambda: g.vector.tensor_scalar(o[0], i[0], a1, None, op0), [o], [i] + sc)
+        else:
+            do("V", lambda: g.vector.tensor_scalar(o[0], i[0], a1, a2, op0, op1), [o], [i] + sc)
+
+    def tt(o, a, b, op):
+        do("V", lambda: g.vector.tensor_tensor(o[0], a[0], b[0], op), [o], [a, b])
+
+    def cp(o, i):
+        do("V", lambda: g.vector.tensor_copy(o[0], i[0]), [o], [i])
+
+    def act(o, i, func, bias=0.0, scale=1.0, acc=None):
+        cols = [s for s in (bias, scale) if isinstance(s, tuple)]
+        b = bias[0] if isinstance(bias, tuple) else bias
+        s = scale[0] if isinstance(scale, tuple) else scale
+        if acc is None:
+            do("S", lambda: g.scalar.activation(o[0], i[0], func, bias=b, scale=s), [o], [i] + cols)
+        else:
+            do("S", lambda: g.scalar.activation(o[0], i[0], func, bias=b, scale=s, accum_out=acc[0]), [o, acc], [i] + cols)
+
+    def scan(o, d0, d1, init):
+        s = [init] if isinstance(init, tuple) else []
+        v = init[0] if isinstance(init, tuple) else init
+        do("V", lambda: g.vector.tensor_tensor_scan(o[0], d0[0], d1[0], v, Op.mult, Op.add), [o], [d0, d1] + s)
+
+    def mm(o, l, rh, start=True, stop=True):
+        do("T", lambda: g.tensor.matmul(o[0], l[0], rh[0], start, stop), [o], [l, rh])
+
+    def iota(o, pattern, base, cm):
+        do("G", lambda: g.iota(o[0], pattern, base, cm, allow_small_or_imprecise_dtypes=True), [o], [])
+
+    def gather(q, o, win, off):
+        if q == "V":
+            do(q, lambda: g.vector.tensor_copy(o[0], win[0].indirect(off[0])), [o], [win, off])
+        else:
+            do(q, lambda: g.scalar.activation(o[0], win[0].indirect(off[0]), Act.Copy), [o], [win, off])
+
+    peers = [(r + k) % N for k in range(1, N)]
+    sibs = [d for d in peers if topo.chip(T.cores[d]) == topo.chip(core)]
+    far = [d for d in peers if d not in sibs]
+    offm = topo.mask(core, T.cores[far[0]])
+    nearm = topo.mask(core, T.cores[sibs[0]]) & ~offm
+    offbits = [1 << i for i in range(16) if offm >> i & 1]
+    neng = lambda m: bin(m).count("1")
+
+    def dst(d):
+        rid, pid, _ = topo.addr(T.cores[d])
+        return DstId(rid=rid, pnc=pid)
+
+    g.sync.dma_start(T.key16[:], T.key[:]).then_inc(T.sem.key, 16)
+    note("key", 16, "dkey", [A("key16")], [])
+    g.sync.dma_start(T.xb[:], T.x[:]).then_inc(T.sem.x, 16)
+    note("x", 16, "dx", [A("xb")], [])
+
+    iota(A("pcol"), [[0, 1]], 0, 1)
+    iota(A("iow"), [[1, 258]], 0, 0)
+    iota(A("p112"), [[0, 1]], 112, 1)
+    iota(A("io16"), [[0, 16], [1, 16]], 0, 0)
+    iota(A("jv"), [[128, 16]], 0, 1)
+    iota(A("pint"), [[0, 1]], 0, 1)
+    iota(A("io32"), [[16, 32]], 0, 0)
+    do("V", lambda: g.vector.memset(T.ph[:, 0:1], 0.0), [A("ph", 0, 1)], [])
+    w128 = A("iow", 0, 128)
+    ts(A("idf"), A("iow", 0, 16, p=16), A("pcol", p=16), Op.is_equal)
+    ts(A("ones"), A("iow"), 0.0, Op.is_ge)
+    for b in range(16):
+        o = A("rowsel", 128 * b, 128 * b + 128)
+        if b % 2 or b > 8:
+            act(o, A("ones", 0, 128, p=16), Act.Copy, scale=A("idf", b, b + 1))
+        else:
+            ts(o, A("ones", 0, 128, p=16), A("idf", b, b + 1), Op.mult)
+        if b == 0:
+            ts(A("z16"), A("iow", 0, 240, p=16), A("p112", p=16), Op.is_equal)
+            ts(A("ident"), w128, A("pcol"), Op.is_equal)
+            for q in range(4):
+                ts(A("pen", 128 * q, 128 * q + 128), w128, A("pcol"), Op.is_le, 0.25, Op.mult)
+            mm(A("kb0"), A("ident"), A("pen"), True, False)
+    cp(A("kd", 0, 128), A("key16"))
+    ts(A("kint", 0, 128), A("key16"), 4, Op.arith_shift_right)
+    ts(A("kint", 128, 256), A("key16"), 15, Op.bitwise_and)
+    for c in range(8):
+        mm(A("pk", 64 + 16 * c, 80 + 16 * c, p=16), A("kd", c, 128, 8), A("z16", 112, 128))
+    cp(A("kd", 128, 256), A("kint", 0, 128))
+    ts(A("kd", 256, 384), A("kint", 128, 256), -1.0, Op.mult)
+    for c in range(8):
+        mm(A("pt", 0, 48), A("z16", 112 - 16 * c, 240 - 16 * c), A("kd", c, 384, 8), c == 0, c == 7)
+    act(A("ktt"), A("pk", 64, 192, p=16), Act.Copy)
+    cp(A("ktd"), A("pt", 0, 48))
+
+    def keyrows(q):
+        if q:
+            mm(A("kb%d" % q), A("ident"), A("pen"), True, False)
+        for b in range(4 * q, 4 * q + 4):
+            mm(A("kb%d" % q, 128 * (b % 4), 128 * (b % 4) + 128), A("rowsel", 128 * b, 128 * b + 128), A("ktt"), False, b % 4 == 3)
+
+    def absrow(q):
+        act(A("kabs", 512 * q, 512 * q + 512), A("kb%d" % q), Act.Abs, bias=A("abias"))
+
+    def equal(q):
+        for b in range(4 * q, 4 * q + 4):
+            ts(A("eq", 128 * b, 128 * b + 128), A("kb%d" % q, 128 * (b % 4), 128 * (b % 4) + 128), A("ktd", b, b + 1), Op.is_equal)
+
+    for b in range(8):
+        act(A("fabs", 16 * b, 16 * b + 16), A("iow", 0, 16), Act.Abs, bias=A("ktd", 32 + b, 33 + b))
+    act(A("ohf", 0, 128), A("fabs", 0, 128), Act.Relu, bias=A("ones", 0, 1), scale=-1.0)
+    for b in range(16):
+        ts(A("oha", 128 * b, 128 * b + 128), w128, A("ktd", 16 + b, 17 + b), Op.is_equal)
+    for b in range(8, 16):
+        ts(A("ohf", 16 * b, 16 * b + 16), A("iow", 0, 16), A("ktd", 32 + b, 33 + b), Op.add, 0.0, Op.is_equal)
+    ts(A("abias"), A("pcol"), -16.0, Op.mult, -7.5, Op.add)
+    keyrows(0)
+    keyrows(1)
+    for b in range(16):
+        mm(A("ph", 1 + b, 242 + b, 16), A("oha", 128 * b, 128 * b + 128), A("ohf", 16 * b, 16 * b + 16))
+    absrow(0)
+    equal(0)
+    ts(A("lst"), w128, A("pcol"), Op.is_gt)
+    scan(A("scan0"), A("ones", 0, 257), A("ph", 0, 257), 0.0)
+    tt(A("hs"), A("scan0", 16, 257, 16), A("scan0", 0, 241, 16), Op.subtract)
+    guard("G", [], [A("hs")])
+    g.remote_dma_fused([RemoteDMATransfer(dst_ids=[dst(d) for d in peers], dma_engine_mask=offm, remote_sem=T.sem.hist,
+                                          srcs=[T.hs[:]], dsts=[T.hl[:, 16 * r:16 * r + 16]] * len(peers))], local_sem=T.sem.loc)
+    nloc = [neng(offm)]
+    for d in peers:
+        note("hist", neng(offm) * len(peers), "rh", [A("hl", 16 * d, 16 * d + 16)], [])
+    keyrows(2)
+    mm(A("pk", 0, 1), A("lst"), A("scan0", 256, 257))
+    keyrows(3)
+    absrow(1)
+    equal(1)
+    ts(A("tbl"), A("scan0", 0, 256), A("pk", 0, 1), Op.add)
+    absrow(2)
+    equal(2)
+    ts(A("oht", 0, 1024), A("kabs", 0, 1024), 8.0, Op.is_lt)
+    absrow(3)
+    equal(3)
+    ts(A("oht", 1024, 2048), A("kabs", 1024, 2048), 8.0, Op.is_lt)
+    ts(A("segm"), A("io16"), 0.0, Op.is_gt)
+    for b in range(16):
+        mm(A("pl", 16 * b, 16 * b + 16), A("oht", 128 * b, 128 * b + 128), A("tbl", b, 241 + b, 16))
+    for b in range(16):
+        mm(A("pt", 256 + b, 257 + b), A("eq", 128 * b, 128 * b + 128), A("ones", 0, 1))
+    tt(A("prod"), A("pl", 0, 256), A("ohf"), Op.mult)
+    scan(A("scan"), A("segm"), A("prod"), 0.0)
+    ts(A("pbit", 0, 1), A("pint"), 15, Op.bitwise_and)
+    ts(A("pbit", 1, 2), A("pint"), 4, Op.arith_shift_right)
+    cp(A("pdig"), A("pbit"))
+    ts(A("hp", 0, 1), A("iow", 0, 1), 0.0, Op.mult)
+    ts(A("onesf"), w128, 0.0, Op.is_ge)
+    for d in range(N):
+        act(A("hrep", 16 * d, 16 * d + 16), A("hs"), Act.Copy)
+    cp(A("hl", 16 * r, 16 * r + 16), A("hs"))
+    ts(A("io32"), A("io32"), A("pdig", 0, 1), Op.add)
+    tt(A("lr"), A("scan", 15, 256, 16), A("pt", 256, 272), Op.add)
+
+    def digits(v, bits, di, df, mu, mo):
+        n = float(1 << bits)
+        ts(A(di), A(v), 1.0 / n, Op.mult, -0.5 + 0.5 / n, Op.add)
+        ts(A(mu), A(di), n, Op.mult)
+        cp(A(df), A(di))
+        tt(A(mo), A(v), A(mu), Op.subtract)
+
+    digits("lr", 4, "divi", "divf", "dmul", "modf")
+    for b in range(16):
+        o = 128 * b
+        ts(A("sl", o, o + 128), A("io16", 0, 128), A("modf", b, b + 1), Op.is_equal)
+        ts(A("sr", o, o + 128), w128, A("divf", b, b + 1), Op.is_equal, A("jv", b, b + 1), Op.mult)
+        mm(A("pt", 0, 128), A("sl", o, o + 128), A("sr", o, o + 128), b == 0, b == 15)
+    cp(A("slist"), A("pt", 0, 128))
+    act(A("junk"), A("hl"), Act.Copy, scale=-1.0, acc=A("rowt", 1, 2))
+    for d in range(N):
+        act(A("hp", 1 + d, 152 + d, 10), A("hl", 16 * d, 16 * d + 16), Act.Copy, scale=-1.0)
+    gather("S", A("xs", 0, XS), A("xb"), A("slist", 0, XS // 16))
+    mm(A("pk", 1, 2), A("lst"), A("rowt", 1, 2))
+    scan(A("base"), A("ones", 0, 160), A("hp", 0, 160), A("pk", 1, 2))
+    own = A("base", r, 151 + r, 10)
+    for d in range(N):
+        ts(A("xr", 16 * d, 16 * d + 16), own, 2048.0 * d, Op.add, 0.0, Op.max)
+    tt(A("xm"), A("xr"), A("hrep"), Op.min)
+    tt(A("dt"), own, A("tbl", 0, 241, 16), Op.add)
+    cp(A("dh"), A("dt"))
+    tt(A("dl"), A("dt"), A("dh"), Op.subtract)
+    mm(A("pk", 16, 176), A("onesf"), A("xm"))
+    scan(A("scb"), A("segm", 0, 160), A("pk", 16, 176), 0.0)
+    bcol = lambda d: A("scb", 16 * d + 15, 16 * d + 16)
+    onS, onV = peers[:NS], peers[NS:]
+    for d in peers + [r]:
+        ts(A("wl", 32 * d, 32 * d + 32), A("io32"), bcol(d), Op.add, 2047.0, Op.min)
+    gather("V", A("xs", XS, NT), A("xb"), A("slist", XS // 16, NT // 16))
+
+    def window(q, d):
+        o = A("wnd", CAP * d, CAP * d + CAP) if d != r else A("ld", CAP * d, CAP * d + CAP)
+        gather(q, o, A("xs"), A("wl", 32 * d, 32 * d + 32))
+
+    def send(d):
+        m = nearm if d in sibs else offm
+        guard("G", [], [A("wnd", CAP * d, CAP * d + CAP)])
+        rid, pid, _ = topo.addr(T.cores[d])
+        g.remote_dma(T.ld[:, CAP * r:CAP * r + CAP], T.wnd[:, CAP * d:CAP * d + CAP], T.sem.dat, T.sem.loc, pid, rid, m)
+        nloc[0] += neng(m)
+
+    for d in onS:
+        window("S", d)
+    for d in onS[:NMAP]:
+        send(d)
+    for b in range(16):
+        o = A("ph", 16 * b, 16 * b + 16)
+        mm(o, A("oht", 128 * b, 128 * b + 128), A("dh"), True, False)
+        mm(o, A("oht", 128 * b, 128 * b + 128), A("dl"), False, True)
+    tt(A("prod2"), A("ph", 0, 256), A("ohf"), Op.mult)
+    scan(A("scan2"), A("segm"), A("prod2"), 0.0)
+    ts(A("lr1"), A("lr"), 1.0, Op.add)
+    tt(A("pos"), A("lr"), A("scan2", 15, 256, 16), Op.subtract)
+    digits("pos", 7, "pdivi", "pdivf", "pmul", "pmod")
+    for b in range(16):
+        ts(A("ml", 128 * b, 128 * b + 128), w128, A("pmod", b, b + 1), Op.is_equal)
+        ts(A("mr", 160 * b, 160 * b + 160), A("iow", 0, 160), A("pdivf", b, b + 1), Op.is_equal, A("lr1", b, b + 1), Op.mult)
+        mm(A("kb0", 0, 160), A("ml", 128 * b, 128 * b + 128), A("mr", 160 * b, 160 * b + 160), b == 0, b == 15)
+    mt = lambda ap: (ap, "mt", 0, 320)
+    for d in range(N):
+        ts(mt(T.mt[:, d, 0:16]), A("kb0", 16 * d, 16 * d + 16), bcol(d), Op.subtract, 0.0, Op.max)
+    ts(mt(T.mt[:, :, 16:32]), mt(T.mt[:, :, 0:16]), 0.0, Op.is_gt, float(CAP * r), Op.mult)
+    guard("G", [], [mt(None)])
+    tr = []
+    for d in peers:
+        m = nearm if d in sibs else offbits[far.index(d) % len(offbits)]
+        tr.append(RemoteDMATransfer(dst_ids=[dst(d)], dma_engine_mask=m, remote_sem=T.sem.map,
+                                    srcs=[T.mt[:, d, 0:32]], dsts=[T.lm[:, 32 * r:32 * r + 32]]))
+        nloc[0] += neng(m)
+        note("map", len(far) + neng(nearm) * len(sibs), "rm", [A("lm", 32 * d, 32 * d + 32)], [])
+    g.remote_dma_fused(tr, local_sem=T.sem.loc)
+    cp(A("lm", 32 * r, 32 * r + 32), mt(T.mt[:, r, 0:32]))
+    for d in onV:
+        window("V", d)
+    for d in onS[NMAP:] + onV:
+        send(d)
+    window("S", r)
+    ts(A("wrap"), A("io16", 0, 128), A("pdig", 0, 1), Op.is_equal)
+    ts(A("m8"), A("iow", 0, 8), A("pdig", 1, 2), Op.is_equal)
+    for c in range(8):
+        ts(A("rl", 128 * c, 128 * c + 128), A("wrap"), A("m8", c, c + 1), Op.mult)
+    for d in peers:
+        note("dat", neng(offm) * len(far) + neng(nearm) * len(sibs), "rd", [A("ld", CAP * d, CAP * d + CAP)], [])
+    tt(A("t1"), A("lm", 0, 160), A("lm", 160, 320), Op.add)
+    tt(A("t2"), A("t1", 0, 64), A("t1", 64, 128), Op.add)
+    tt(A("t3"), A("t2", 0, 32), A("t2", 32, 64), Op.add)
+    tt(A("t4"), A("t3"), A("t1", 128, 160), Op.add)
+    for c in range(8):
+        o = A("kb1", c, 121 + c, 8)
+        mm(o, A("rl", 128 * c, 128 * c + 128), A("t4", 0, 16), True, False)
+        mm(o, A("rl", 128 * c, 128 * c + 128), A("t4", 16, 32), False, True)
+    ts(A("flist"), A("kb1", 0, 128), -1.0, Op.add)
+    for k in range(4):
+        q = "VS"[k % 2]
+        gather(q, A("yb", 512 * k, 512 * k + 512), A("ld"), A("flist", 32 * k, 32 * k + 32))
+        guard("Y", [], [A("yb", 512 * k, 512 * k + 512)])
+        g.sync.dma_start(T.y[:, 512 * k:512 * k + 512], T.yb[:, 512 * k:512 * k + 512]).then_inc(T.sem.st, 16)
+    for q in "VSTG":
+        g.wait_ge(T.sem[q], cnt[q])
+    g.wait_ge(T.sem.key, 16)
+    g.wait_ge(T.sem.x, 16)
+    g.wait_ge(T.sem.loc, nloc[0])
+    g.wait_ge(T.sem.hist, neng(offm) * len(peers))
+    g.wait_ge(T.sem.map, len(far) + neng(nearm) * len(sibs))
+    g.wait_ge(T.sem.dat, neng(offm) * len(far) + neng(nearm) * len(sibs))
+    g.wait_ge(T.sem.st, 64)

@@ -1,9 +1,11 @@
 from concourse.bass import DstId, RemoteDMATransfer
-from concourse.mybir import AluOpType as Op, AxisListType, ActivationFunctionType as Act
+from concourse.mybir import AluOpType as Op, ActivationFunctionType as Act
 
 B16, F16, F32, I32, U16 = "bfloat16", "float16", "float32", "int32", "uint16"
 N, NT, CAP = 10, 2048, 512
-XS, NS, NMAP = 1664, 7, 6
+MAINW, TWINW = (0, 1, 2, 8), (3, 4, 5, 6, 7)
+RELAYW = (3,)
+PARTY = (0, 640, 1280, 1664, 2048)
 SCRATCH = {
     "idf": ("sbuf", [16, 16], F32), "rowsel": ("sbuf", [16, 2048], F16), "z16": ("sbuf", [16, 240], F16),
     "key16": ("sbuf", [16, 128], I32), "kint": ("sbuf", [16, 256], I32), "kd": ("sbuf", [16, 384], F16),
@@ -11,22 +13,22 @@ SCRATCH = {
     "sl": ("sbuf", [128, 2048], F16), "sr": ("sbuf", [128, 2048], F16), "slist": ("sbuf", [128, 128], U16),
     "ml": ("sbuf", [128, 2048], F16), "mr": ("sbuf", [128, 2560], F16), "mt": ("sbuf", [128, 10, 32], F16),
     "hs": ("sbuf", [128, 16], F16), "hl": ("sbuf", [128, 160], F16), "lm": ("sbuf", [128, 320], F16),
-    "wl": ("sbuf", [128, 320], U16), "flist": ("sbuf", [128, 128], U16),
+    "scb": ("sbuf", [128, 160], F32), "wl": ("sbuf", [128, 320], U16), "flist": ("sbuf", [128, 128], U16),
     "xb": ("sbuf", [128, 2048], B16), "xs": ("sbuf", [128, 2048], B16),
     "wnd": ("sbuf", [128, 5120], B16), "ld": ("sbuf", [128, 5120], B16), "yb": ("sbuf", [128, 2048], B16),
 }
 for _k in ("pk", "ph", "pt", "pl", "kb0", "kb1", "kb2", "kb3"):
     SCRATCH[_k] = ("psum", [128, 512], F32)
 PARTS = {
-    ("ff", F32): [("pcol", 1), ("p112", 1), ("pdig", 2), ("io32", 32), ("jv", 16), ("abias", 1), ("m8", 8), ("lst", 128),
+    ("ff", F32): [("pcol", 1), ("pdig", 2), ("io32", 32), ("jv", 16), ("abias", 1), ("m8", 8), ("lst", 128),
                   ("ktd", 48), ("scan0", 257), ("rowt", 2), ("prod", 256), ("scan", 256), ("lr", 16), ("divf", 16),
-                  ("dmul", 16), ("modf", 16), ("base", 160), ("xr", 160), ("scb", 160), ("dt", 16), ("prod2", 256),
+                  ("dmul", 16), ("modf", 16), ("base", 160), ("xr", 160), ("dt", 16), ("prod2", 256),
                   ("scan2", 256), ("pos", 16), ("lr1", 16), ("pdivf", 16), ("pmul", 16), ("pmod", 16)],
     ("ii", I32): [("pint", 1), ("pbit", 2), ("divi", 16), ("pdivi", 16)],
     ("hh", F16): [("ident", 128), ("pen", 512), ("onesf", 128), ("rl", 1024), ("wrap", 128), ("kabs", 2048), ("oht", 2048),
                   ("tbl", 256), ("hp", 176), ("junk", 160), ("hrep", 160), ("xm", 160), ("dh", 16), ("dl", 16),
                   ("t1", 160), ("t2", 64), ("t3", 32), ("t4", 32)],
-    ("bb", B16): [("iow", 258), ("io16", 256), ("ones", 258), ("segm", 256), ("fabs", 256), ("oha", 2048), ("ohf", 256),
+    ("bb", B16): [("iow", 160), ("io16", 256), ("ones", 258), ("segm", 256), ("fabs", 256), ("oha", 2048), ("ohf", 256),
                   ("eq", 2048)],
 }
 ALIAS = {}
@@ -36,13 +38,33 @@ for (_b, _d), _l in PARTS.items():
         ALIAS[_n] = (_b, _o, _w)
         _o += _w
     SCRATCH[_b] = ("sbuf", [128, _o], _d)
-SEMAPHORES = ["V", "S", "T", "G", "key", "x", "st", "hist", "map", "dat", "loc"]
+SEMAPHORES = ["V", "S", "T", "G", "key", "x", "st", "hist", "map", "dat", "loc", "tx", "tl", "tw"] + ["hop%d" % _i for _i in range(len(RELAYW))]
 
 
 def rank_program(g, core, T, topo):
     r = T.rank_of(core)
-    if r is None:
-        return
+    neng = lambda m: bin(m).count("1")
+    near = lambda a, b: topo.chip(T.cores[a]) == topo.chip(T.cores[b])
+
+    def order(q):
+        rot = [(q + k) % N for k in range(1, N)]
+        return [d for d in rot if not near(q, d)] + [d for d in rot if near(q, d)]
+
+    last = topo.chip(max(T.cores))
+    ncore = max(T.cores) + 1
+    while topo.chip(ncore) == last or topo.mates(topo.chip(ncore), last):
+        ncore += 1
+
+    def relay(q, k):
+        c = T.cores[order(q)[k]]
+        own = [h for h in range(ncore) if topo.mates(topo.chip(h), topo.chip(c)) and topo.die(h) == topo.die(T.cores[q]) and topo.may_write(h, c)]
+        return own[RELAYW.index(k) % len(own)]
+
+    def twin(q):
+        c, p = T.cores[q], relay(q, RELAYW[0])
+        return [h for h in range(ncore) if topo.chip(h) == topo.chip(c) and topo.die(h) == topo.die(c) and T.rank_of(h) is None
+                and topo.may_write(h, p)][0]
+
     eng = {"V": g.vector, "S": g.scalar, "T": g.tensor, "G": g, "Y": g.sync}
     log, seen, cnt = {}, {}, {}
 
@@ -82,8 +104,8 @@ def rank_program(g, core, T, topo):
         fn().then_inc(T.sem[q], 1)
         note(q, cnt[q], q, outs, ins)
 
-    def ts(o, i, s1, op0, s2=None, op1=None):
-        sc = [s for s in (s1, s2) if isinstance(s, tuple)]
+    def ts(o, i, s1, op0, s2=None, op1=None, after=()):
+        sc = [s for s in (s1, s2) if isinstance(s, tuple)] + list(after)
         a1 = s1[0] if isinstance(s1, tuple) else s1
         a2 = s2[0] if isinstance(s2, tuple) else s2
         if op1 is None:
@@ -96,6 +118,9 @@ def rank_program(g, core, T, topo):
 
     def cp(o, i):
         do("V", lambda: g.vector.tensor_copy(o[0], i[0]), [o], [i])
+
+    def fill(o, c):
+        do("V", lambda: g.vector.memset(o[0], c), [o], [])
 
     def act(o, i, func, bias=0.0, scale=1.0, acc=None):
         cols = [s for s in (bias, scale) if isinstance(s, tuple)]
@@ -123,17 +148,81 @@ def rank_program(g, core, T, topo):
         else:
             do(q, lambda: g.scalar.activation(o[0], win[0].indirect(off[0]), Act.Copy), [o], [win, off])
 
-    peers = [(r + k) % N for k in range(1, N)]
-    sibs = [d for d in peers if topo.chip(T.cores[d]) == topo.chip(core)]
-    far = [d for d in peers if d not in sibs]
+    bcol = lambda d: A("scb", 16 * d + 15, 16 * d + 16)
+    wslot = lambda d: A("wnd", CAP * d, CAP * d + CAP)
+    nloc = [0]
+
+    def groupcols():
+        ts(A("pbit", 0, 1), A("pint"), 15, Op.bitwise_and)
+        ts(A("pbit", 1, 2), A("pint"), 4, Op.arith_shift_right)
+        cp(A("pdig"), A("pbit"))
+        ts(A("io32"), A("io32"), A("pdig", 0, 1), Op.add)
+
+    def offsets(d):
+        ts(A("wl", 32 * d, 32 * d + 32), A("io32"), bcol(d), Op.add, NT - 1.0, Op.min)
+
+    def window(q, d, o):
+        gather(q, o, A("xs"), A("wl", 32 * d, 32 * d + 32))
+
+    def write(out, in_, sem, to, m):
+        rid, pid, _ = topo.addr(to)
+        g.remote_dma(out, in_, T.sem[sem], T.sem.loc, pid, rid, m)
+        nloc[0] += neng(m)
+
+    def send(q, d, m, src=None):
+        guard("G", [], [wslot(d)] if src is None else [])
+        write(T.ld[:, CAP * q:CAP * q + CAP], wslot(d)[0] if src is None else src, "dat", T.cores[d], m)
+
+    passed = lambda i: T.wnd[:, CAP * i:CAP * i + CAP]
+    if r is None:
+        for q in range(N):
+            if twin(q) != core:
+                continue
+            ds = [order(q)[k] for k in TWINW]
+            nm = neng(topo.mask(T.cores[q], core) & ~topo.mask(T.cores[q], T.cores[ds[0]]))
+            for sem, buf in (("tx", "xb"), ("tl", "slist"), ("tw", "scb")):
+                note(sem, nm, sem, [A(buf)], [])
+            iota(A("pint"), [[0, 1]], 0, 1)
+            iota(A("io32"), [[16, 32]], 0, 0)
+            groupcols()
+            gather("S", A("xs", 0, 1024), A("xb"), A("slist", 0, 64))
+            gather("V", A("xs", 1024, 2048), A("xb"), A("slist", 64, 128))
+            for d in ds:
+                offsets(d)
+            for n, (k, d) in enumerate(zip(TWINW, ds)):
+                window("VS"[n % 2], d, wslot(d))
+                if k in RELAYW:
+                    i, h = RELAYW.index(k), relay(q, k)
+                    guard("G", [], [wslot(d)])
+                    write(passed(i), wslot(d)[0], "hop%d" % i, h, topo.mask(core, h))
+                else:
+                    send(q, d, topo.mask(core, T.cores[d]))
+            for sem, c in (("V", cnt["V"]), ("S", cnt["S"]), ("G", cnt["G"]), ("tx", nm), ("tl", nm), ("tw", nm)):
+                g.wait_ge(T.sem[sem], c)
+        for i, k in enumerate(RELAYW):
+            for q in range(N):
+                if relay(q, k) == core:
+                    d = order(q)[k]
+                    g.wait_ge(T.sem["hop%d" % i], neng(topo.mask(twin(q), core)))
+                    send(q, d, topo.mask(core, T.cores[d]), passed(i))
+        if nloc[0]:
+            g.wait_ge(T.sem.loc, nloc[0])
+        return
+
+    peers = order(r)
+    sibs = [d for d in peers if near(r, d)]
+    far = [d for d in peers if not near(r, d)]
     offm = topo.mask(core, T.cores[far[0]])
     nearm = topo.mask(core, T.cores[sibs[0]]) & ~offm
     offbits = [1 << i for i in range(16) if offm >> i & 1]
-    neng = lambda m: bin(m).count("1")
 
     def dst(d):
         rid, pid, _ = topo.addr(T.cores[d])
         return DstId(rid=rid, pnc=pid)
+
+    def share(buf, sem):
+        guard("G", [], [A(buf)])
+        write(T[buf][:], T[buf][:], sem, twin(r), nearm)
 
     g.sync.dma_start(T.key16[:], T.key[:]).then_inc(T.sem.key, 16)
     note("key", 16, "dkey", [A("key16")], [])
@@ -141,28 +230,31 @@ def rank_program(g, core, T, topo):
     note("x", 16, "dx", [A("xb")], [])
 
     iota(A("pcol"), [[0, 1]], 0, 1)
-    iota(A("iow"), [[1, 258]], 0, 0)
-    iota(A("p112"), [[0, 1]], 112, 1)
+    iota(A("iow"), [[1, 160]], 0, 0)
     iota(A("io16"), [[0, 16], [1, 16]], 0, 0)
     iota(A("jv"), [[128, 16]], 0, 1)
     iota(A("pint"), [[0, 1]], 0, 1)
     iota(A("io32"), [[16, 32]], 0, 0)
-    do("V", lambda: g.vector.memset(T.ph[:, 0:1], 0.0), [A("ph", 0, 1)], [])
+    fill(A("ones"), 1.0)
+    fill(A("ph", 0, 1), 0.0)
+    ts(A("z16"), A("ones", 0, 240, p=16), 0.0, Op.mult)
+    ts(A("hp", 0, 1), A("ones", 0, 1), 0.0, Op.mult)
+    cp(A("onesf"), A("ones", 0, 128))
+    ts(A("abias"), A("pcol"), -16.0, Op.mult, -7.5, Op.add)
     w128 = A("iow", 0, 128)
+    ts(A("ident"), w128, A("pcol"), Op.is_equal)
+    for q in range(4):
+        ts(A("pen", 128 * q, 128 * q + 128), w128, A("pcol"), Op.is_le, 0.25, Op.mult)
+    for q in range(2):
+        mm(A("kb%d" % q), A("ident"), A("pen"), True, False)
     ts(A("idf"), A("iow", 0, 16, p=16), A("pcol", p=16), Op.is_equal)
-    ts(A("ones"), A("iow"), 0.0, Op.is_ge)
+    ts(A("z16", 112, 128), A("iow", 0, 16, p=16), A("pcol", p=16), Op.is_equal, after=[A("z16", 112, 128)])
     for b in range(16):
         o = A("rowsel", 128 * b, 128 * b + 128)
         if b % 2 or b > 8:
             act(o, A("ones", 0, 128, p=16), Act.Copy, scale=A("idf", b, b + 1))
         else:
             ts(o, A("ones", 0, 128, p=16), A("idf", b, b + 1), Op.mult)
-        if b == 0:
-            ts(A("z16"), A("iow", 0, 240, p=16), A("p112", p=16), Op.is_equal)
-            ts(A("ident"), w128, A("pcol"), Op.is_equal)
-            for q in range(4):
-                ts(A("pen", 128 * q, 128 * q + 128), w128, A("pcol"), Op.is_le, 0.25, Op.mult)
-            mm(A("kb0"), A("ident"), A("pen"), True, False)
     cp(A("kd", 0, 128), A("key16"))
     ts(A("kint", 0, 128), A("key16"), 4, Op.arith_shift_right)
     ts(A("kint", 128, 256), A("key16"), 15, Op.bitwise_and)
@@ -176,13 +268,16 @@ def rank_program(g, core, T, topo):
     cp(A("ktd"), A("pt", 0, 48))
 
     def keyrows(q):
-        if q:
+        if q > 1:
             mm(A("kb%d" % q), A("ident"), A("pen"), True, False)
         for b in range(4 * q, 4 * q + 4):
             mm(A("kb%d" % q, 128 * (b % 4), 128 * (b % 4) + 128), A("rowsel", 128 * b, 128 * b + 128), A("ktt"), False, b % 4 == 3)
 
     def absrow(q):
         act(A("kabs", 512 * q, 512 * q + 512), A("kb%d" % q), Act.Abs, bias=A("abias"))
+
+    def digitrow(lo, hi):
+        ts(A("oht", lo, hi), A("kabs", lo, hi), 8.0, Op.is_lt)
 
     def equal(q):
         for b in range(4 * q, 4 * q + 4):
@@ -195,7 +290,6 @@ def rank_program(g, core, T, topo):
         ts(A("oha", 128 * b, 128 * b + 128), w128, A("ktd", 16 + b, 17 + b), Op.is_equal)
     for b in range(8, 16):
         ts(A("ohf", 16 * b, 16 * b + 16), A("iow", 0, 16), A("ktd", 32 + b, 33 + b), Op.add, 0.0, Op.is_equal)
-    ts(A("abias"), A("pcol"), -16.0, Op.mult, -7.5, Op.add)
     keyrows(0)
     keyrows(1)
     for b in range(16):
@@ -206,39 +300,53 @@ def rank_program(g, core, T, topo):
     scan(A("scan0"), A("ones", 0, 257), A("ph", 0, 257), 0.0)
     tt(A("hs"), A("scan0", 16, 257, 16), A("scan0", 0, 241, 16), Op.subtract)
     guard("G", [], [A("hs")])
-    g.remote_dma_fused([RemoteDMATransfer(dst_ids=[dst(d) for d in peers], dma_engine_mask=offm, remote_sem=T.sem.hist,
-                                          srcs=[T.hs[:]], dsts=[T.hl[:, 16 * r:16 * r + 16]] * len(peers))], local_sem=T.sem.loc)
-    nloc = [neng(offm)]
+    for ds, m in ((far, offm), (sibs, nearm)):
+        g.remote_dma_fused([RemoteDMATransfer(dst_ids=[dst(d) for d in ds], dma_engine_mask=m, remote_sem=T.sem.hist, srcs=[T.hs[:]],
+                                              dsts=[T.hl[:, 16 * r:16 * r + 16]] * len(ds))], local_sem=T.sem.loc)
+        nloc[0] += neng(m)
+    nhist = neng(offm) * len(far) + neng(nearm) * len(sibs)
     for d in peers:
-        note("hist", neng(offm) * len(peers), "rh", [A("hl", 16 * d, 16 * d + 16)], [])
+        note("hist", nhist, "rh", [A("hl", 16 * d, 16 * d + 16)], [])
+    share("xb", "tx")
     keyrows(2)
     mm(A("pk", 0, 1), A("lst"), A("scan0", 256, 257))
     keyrows(3)
     absrow(1)
     equal(1)
+    digitrow(0, 1024)
     ts(A("tbl"), A("scan0", 0, 256), A("pk", 0, 1), Op.add)
     absrow(2)
     equal(2)
-    ts(A("oht", 0, 1024), A("kabs", 0, 1024), 8.0, Op.is_lt)
-    absrow(3)
-    equal(3)
-    ts(A("oht", 1024, 2048), A("kabs", 1024, 2048), 8.0, Op.is_lt)
-    ts(A("segm"), A("io16"), 0.0, Op.is_gt)
-    for b in range(16):
-        mm(A("pl", 16 * b, 16 * b + 16), A("oht", 128 * b, 128 * b + 128), A("tbl", b, 241 + b, 16))
-    for b in range(16):
-        mm(A("pt", 256 + b, 257 + b), A("eq", 128 * b, 128 * b + 128), A("ones", 0, 1))
-    tt(A("prod"), A("pl", 0, 256), A("ohf"), Op.mult)
-    scan(A("scan"), A("segm"), A("prod"), 0.0)
-    ts(A("pbit", 0, 1), A("pint"), 15, Op.bitwise_and)
-    ts(A("pbit", 1, 2), A("pint"), 4, Op.arith_shift_right)
-    cp(A("pdig"), A("pbit"))
-    ts(A("hp", 0, 1), A("iow", 0, 1), 0.0, Op.mult)
-    ts(A("onesf"), w128, 0.0, Op.is_ge)
+    groupcols()
     for d in range(N):
         act(A("hrep", 16 * d, 16 * d + 16), A("hs"), Act.Copy)
     cp(A("hl", 16 * r, 16 * r + 16), A("hs"))
-    ts(A("io32"), A("io32"), A("pdig", 0, 1), Op.add)
+    digitrow(1024, 1536)
+    ts(A("segm"), A("io16"), 0.0, Op.is_gt)
+    absrow(3)
+    digitrow(1536, 2048)
+    equal(3)
+    half = lambda h: A("pl" if h == 0 else "ph", 0, 128)
+
+    def lookup(h):
+        for b in range(8 * h, 8 * h + 8):
+            o = A("pl" if h == 0 else "ph", 16 * (b % 8), 16 * (b % 8) + 16)
+            mm(o, A("oht", 128 * b, 128 * b + 128), A("tbl", b, 241 + b, 16))
+
+    def count(lo, hi):
+        for b in range(lo, hi):
+            mm(A("pt", 256 + b, 257 + b), A("eq", 128 * b, 128 * b + 128), A("ones", 0, 1))
+
+    def pick(prod, out, h):
+        tt(A(prod, 128 * h, 128 * h + 128), half(h), A("ohf", 128 * h, 128 * h + 128), Op.mult)
+        scan(A(out, 128 * h, 128 * h + 128), A("segm", 0, 128), A(prod, 128 * h, 128 * h + 128), 0.0)
+
+    lookup(0)
+    count(0, 12)
+    lookup(1)
+    count(12, 16)
+    pick("prod", "scan", 0)
+    pick("prod", "scan", 1)
     tt(A("lr"), A("scan", 15, 256, 16), A("pt", 256, 272), Op.add)
 
     def digits(v, bits, di, df, mu, mo):
@@ -255,49 +363,43 @@ def rank_program(g, core, T, topo):
         ts(A("sr", o, o + 128), w128, A("divf", b, b + 1), Op.is_equal, A("jv", b, b + 1), Op.mult)
         mm(A("pt", 0, 128), A("sl", o, o + 128), A("sr", o, o + 128), b == 0, b == 15)
     cp(A("slist"), A("pt", 0, 128))
+    share("slist", "tl")
     act(A("junk"), A("hl"), Act.Copy, scale=-1.0, acc=A("rowt", 1, 2))
     for d in range(N):
         act(A("hp", 1 + d, 152 + d, 10), A("hl", 16 * d, 16 * d + 16), Act.Copy, scale=-1.0)
-    gather("S", A("xs", 0, XS), A("xb"), A("slist", 0, XS // 16))
+    gather("S", A("xs"), A("xb"), A("slist"))
     mm(A("pk", 1, 2), A("lst"), A("rowt", 1, 2))
     scan(A("base"), A("ones", 0, 160), A("hp", 0, 160), A("pk", 1, 2))
     own = A("base", r, 151 + r, 10)
-    for d in range(N):
-        ts(A("xr", 16 * d, 16 * d + 16), own, 2048.0 * d, Op.add, 0.0, Op.max)
-    tt(A("xm"), A("xr"), A("hrep"), Op.min)
     tt(A("dt"), own, A("tbl", 0, 241, 16), Op.add)
     cp(A("dh"), A("dt"))
     tt(A("dl"), A("dt"), A("dh"), Op.subtract)
-    mm(A("pk", 16, 176), A("onesf"), A("xm"))
-    scan(A("scb"), A("segm", 0, 160), A("pk", 16, 176), 0.0)
-    bcol = lambda d: A("scb", 16 * d + 15, 16 * d + 16)
-    onS, onV = peers[:NS], peers[NS:]
-    for d in peers + [r]:
-        ts(A("wl", 32 * d, 32 * d + 32), A("io32"), bcol(d), Op.add, 2047.0, Op.min)
-    gather("V", A("xs", XS, NT), A("xb"), A("slist", XS // 16, NT // 16))
 
-    def window(q, d):
-        o = A("wnd", CAP * d, CAP * d + CAP) if d != r else A("ld", CAP * d, CAP * d + CAP)
-        gather(q, o, A("xs"), A("wl", 32 * d, 32 * d + 32))
+    def places(h):
+        for b in range(8 * h, 8 * h + 8):
+            o = A("pl" if h == 0 else "ph", 16 * (b % 8), 16 * (b % 8) + 16)
+            mm(o, A("oht", 128 * b, 128 * b + 128), A("dh"), True, False)
+            mm(o, A("oht", 128 * b, 128 * b + 128), A("dl"), False, True)
 
-    def send(d):
-        m = nearm if d in sibs else offm
-        guard("G", [], [A("wnd", CAP * d, CAP * d + CAP)])
-        rid, pid, _ = topo.addr(T.cores[d])
-        g.remote_dma(T.ld[:, CAP * r:CAP * r + CAP], T.wnd[:, CAP * d:CAP * d + CAP], T.sem.dat, T.sem.loc, pid, rid, m)
-        nloc[0] += neng(m)
-
-    for d in onS:
-        window("S", d)
-    for d in onS[:NMAP]:
-        send(d)
-    for b in range(16):
-        o = A("ph", 16 * b, 16 * b + 16)
-        mm(o, A("oht", 128 * b, 128 * b + 128), A("dh"), True, False)
-        mm(o, A("oht", 128 * b, 128 * b + 128), A("dl"), False, True)
-    tt(A("prod2"), A("ph", 0, 256), A("ohf"), Op.mult)
-    scan(A("scan2"), A("segm"), A("prod2"), 0.0)
+    places(0)
+    for d in range(N):
+        ts(A("xr", 16 * d, 16 * d + 16), own, 2048.0 * d, Op.add, 0.0, Op.max)
+    tt(A("xm"), A("xr"), A("hrep"), Op.min)
     ts(A("lr1"), A("lr"), 1.0, Op.add)
+    pick("prod2", "scan2", 0)
+    mm(A("pk", 16, 176), A("onesf"), A("xm"))
+    places(1)
+    scan(A("scb"), A("segm", 0, 160), A("pk", 16, 176), 0.0)
+    share("scb", "tw")
+    mine = [peers[k] for k in MAINW]
+    for d in mine + [r]:
+        offsets(d)
+    for d in mine:
+        window("S", d, wslot(d))
+        if d in far:
+            send(r, d, offm)
+    window("S", r, A("ld", CAP * r, CAP * r + CAP))
+    pick("prod2", "scan2", 1)
     tt(A("pos"), A("lr"), A("scan2", 15, 256, 16), Op.subtract)
     digits("pos", 7, "pdivi", "pdivf", "pmul", "pmod")
     for b in range(16):
@@ -309,26 +411,25 @@ def rank_program(g, core, T, topo):
         ts(mt(T.mt[:, d, 0:16]), A("kb0", 16 * d, 16 * d + 16), bcol(d), Op.subtract, 0.0, Op.max)
     ts(mt(T.mt[:, :, 16:32]), mt(T.mt[:, :, 0:16]), 0.0, Op.is_gt, float(CAP * r), Op.mult)
     guard("G", [], [mt(None)])
+    nmap = len(far) + neng(nearm) * len(sibs)
     tr = []
     for d in peers:
         m = nearm if d in sibs else offbits[far.index(d) % len(offbits)]
         tr.append(RemoteDMATransfer(dst_ids=[dst(d)], dma_engine_mask=m, remote_sem=T.sem.map,
                                     srcs=[T.mt[:, d, 0:32]], dsts=[T.lm[:, 32 * r:32 * r + 32]]))
         nloc[0] += neng(m)
-        note("map", len(far) + neng(nearm) * len(sibs), "rm", [A("lm", 32 * d, 32 * d + 32)], [])
+        note("map", nmap, "rm", [A("lm", 32 * d, 32 * d + 32)], [])
     g.remote_dma_fused(tr, local_sem=T.sem.loc)
     cp(A("lm", 32 * r, 32 * r + 32), mt(T.mt[:, r, 0:32]))
-    for d in onV:
-        window("V", d)
-    for d in onS[NMAP:] + onV:
-        send(d)
-    window("S", r)
+    for d in sibs:
+        send(r, d, nearm)
     ts(A("wrap"), A("io16", 0, 128), A("pdig", 0, 1), Op.is_equal)
     ts(A("m8"), A("iow", 0, 8), A("pdig", 1, 2), Op.is_equal)
     for c in range(8):
         ts(A("rl", 128 * c, 128 * c + 128), A("wrap"), A("m8", c, c + 1), Op.mult)
+    got = neng(offm) * len(far) + neng(nearm) * len(sibs)
     for d in peers:
-        note("dat", neng(offm) * len(far) + neng(nearm) * len(sibs), "rd", [A("ld", CAP * d, CAP * d + CAP)], [])
+        note("dat", got, "rd", [A("ld", CAP * d, CAP * d + CAP)], [])
     tt(A("t1"), A("lm", 0, 160), A("lm", 160, 320), Op.add)
     tt(A("t2"), A("t1", 0, 64), A("t1", 64, 128), Op.add)
     tt(A("t3"), A("t2", 0, 32), A("t2", 32, 64), Op.add)
@@ -338,17 +439,10 @@ def rank_program(g, core, T, topo):
         mm(o, A("rl", 128 * c, 128 * c + 128), A("t4", 0, 16), True, False)
         mm(o, A("rl", 128 * c, 128 * c + 128), A("t4", 16, 32), False, True)
     ts(A("flist"), A("kb1", 0, 128), -1.0, Op.add)
-    for k in range(4):
-        q = "VS"[k % 2]
-        gather(q, A("yb", 512 * k, 512 * k + 512), A("ld"), A("flist", 32 * k, 32 * k + 32))
-        guard("Y", [], [A("yb", 512 * k, 512 * k + 512)])
-        g.sync.dma_start(T.y[:, 512 * k:512 * k + 512], T.yb[:, 512 * k:512 * k + 512]).then_inc(T.sem.st, 16)
-    for q in "VSTG":
-        g.wait_ge(T.sem[q], cnt[q])
-    g.wait_ge(T.sem.key, 16)
-    g.wait_ge(T.sem.x, 16)
-    g.wait_ge(T.sem.loc, nloc[0])
-    g.wait_ge(T.sem.hist, neng(offm) * len(peers))
-    g.wait_ge(T.sem.map, len(far) + neng(nearm) * len(sibs))
-    g.wait_ge(T.sem.dat, neng(offm) * len(far) + neng(nearm) * len(sibs))
-    g.wait_ge(T.sem.st, 64)
+    for n, (lo, hi) in enumerate(zip(PARTY, PARTY[1:])):
+        gather("VS"[n % 2], A("yb", lo, hi), A("ld"), A("flist", lo // 16, hi // 16))
+        guard("Y", [], [A("yb", lo, hi)])
+        g.sync.dma_start(T.y[:, lo:hi], T.yb[:, lo:hi]).then_inc(T.sem.st, 16)
+    for sem, c in [(q, cnt[q]) for q in "VSTG"] + [("key", 16), ("x", 16), ("loc", nloc[0]), ("hist", nhist), ("map", nmap), ("dat", got),
+                                                   ("st", 16 * (len(PARTY) - 1))]:
+        g.wait_ge(T.sem[sem], c)

@@ -2,34 +2,31 @@ from concourse.bass import DstId, RemoteDMATransfer
 from concourse.mybir import AluOpType as Op, ActivationFunctionType as Act
 
 B16, F16, F32, I32, U16 = "bfloat16", "float16", "float32", "int32", "uint16"
-N, NT, CAP = 10, 2048, 512
-MAINW, TWINW = (0, 1, 2, 8), (3, 4, 5, 6, 7)
-RELAYW = (3,)
-PARTY = (0, 640, 1280, 1664, 2048)
+N, NT = 10, 2048
+PIECES = ((0, 144), (144, 288), (288, 1184), (1184, 1616), (1616, 2048))
+WHO = (0, 1, 2, 0, 1)
+EARLY = 3
+FIRST = (2, 0, 1, 3, 4)
+SUBS = ((288, 512), (512, 736), (736, 1184))
+PARTY = (0, 512, 1024, 1312, 1600, 1824, 2048)
 SCRATCH = {
     "idf": ("sbuf", [16, 16], F32), "rowsel": ("sbuf", [16, 2048], F16), "z16": ("sbuf", [16, 240], F16),
-    "key16": ("sbuf", [16, 128], I32), "kint": ("sbuf", [16, 256], I32), "kd": ("sbuf", [16, 384], F16),
-    "ktt": ("sbuf", [16, 128], F16),
-    "sl": ("sbuf", [128, 2048], F16), "sr": ("sbuf", [128, 2048], F16), "slist": ("sbuf", [128, 128], U16),
-    "ml": ("sbuf", [128, 2048], F16), "mr": ("sbuf", [128, 2560], F16), "mt": ("sbuf", [128, 10, 32], F16),
-    "hs": ("sbuf", [128, 16], F16), "hl": ("sbuf", [128, 160], F16), "lm": ("sbuf", [128, 320], F16),
-    "scb": ("sbuf", [128, 160], F32), "wl": ("sbuf", [128, 320], U16), "flist": ("sbuf", [128, 128], U16),
-    "xb": ("sbuf", [128, 2048], B16), "xs": ("sbuf", [128, 2048], B16),
-    "wnd": ("sbuf", [128, 5120], B16), "ld": ("sbuf", [128, 5120], B16), "yb": ("sbuf", [128, 2048], B16),
+    "key16": ("sbuf", [16, 128], I32), "kd": ("sbuf", [16, 128], F16), "ktt": ("sbuf", [16, 128], F16),
+    "ml": ("sbuf", [128, 2048], F16), "mr": ("sbuf", [128, 2560], F16), "mx": ("sbuf", [128, 2560], F32),
+    "mt": ("sbuf", [128, 160], F32), "lm": ("sbuf", [128, 160], F32),
+    "hs": ("sbuf", [128, 16], F16), "hl": ("sbuf", [128, 160], F16), "flist": ("sbuf", [128, 128], U16),
+    "ld": ("sbuf", [128, N * NT], B16), "yb": ("sbuf", [128, 2048], B16),
 }
 for _k in ("pk", "ph", "pt", "pl", "kb0", "kb1", "kb2", "kb3"):
     SCRATCH[_k] = ("psum", [128, 512], F32)
 PARTS = {
-    ("ff", F32): [("pcol", 1), ("pdig", 2), ("io32", 32), ("jv", 16), ("abias", 1), ("m8", 8), ("lst", 128),
-                  ("ktd", 48), ("scan0", 257), ("rowt", 2), ("prod", 256), ("scan", 256), ("lr", 16), ("divf", 16),
-                  ("dmul", 16), ("modf", 16), ("base", 160), ("xr", 160), ("dt", 16), ("prod2", 256),
-                  ("scan2", 256), ("pos", 16), ("lr1", 16), ("pdivf", 16), ("pmul", 16), ("pmod", 16)],
-    ("ii", I32): [("pint", 1), ("pbit", 2), ("divi", 16), ("pdivi", 16)],
-    ("hh", F16): [("ident", 128), ("pen", 512), ("onesf", 128), ("rl", 1024), ("wrap", 128), ("kabs", 2048), ("oht", 2048),
-                  ("tbl", 256), ("hp", 176), ("junk", 160), ("hrep", 160), ("xm", 160), ("dh", 16), ("dl", 16),
-                  ("t1", 160), ("t2", 64), ("t3", 32), ("t4", 32)],
-    ("bb", B16): [("iow", 160), ("io16", 256), ("ones", 258), ("segm", 256), ("fabs", 256), ("oha", 2048), ("ohf", 256),
-                  ("eq", 2048)],
+    ("ff", F32): [("pcol", 1), ("pdig", 2), ("jv1", 16), ("jvn", 16), ("abias", 1), ("m8", 8), ("lst", 128), ("ktd", 16), ("a16", 16),
+                  ("u", 16), ("rowt", 1), ("scan", 528), ("pmul", 16), ("msk", 160), ("t1", 80), ("t2", 32), ("t3", 16), ("t4", 16)],
+    ("ii", I32): [("pint", 1), ("pbit", 2), ("adivi", 16), ("pdivi", 16)],
+    ("hh", F16): [("ident", 128), ("pen", 512), ("rl", 1024), ("wrap", 128), ("kabs", 2048), ("oht", 2048), ("loc", 272),
+                  ("ltab", 256), ("tab", 33), ("junk", 160), ("th", 16), ("tl", 16)],
+    ("bb", B16): [("iow", 160), ("iowk", 160), ("i16", 128), ("io16", 256), ("cm16", 16), ("c33", 34), ("ones", 256), ("zz", 264),
+                  ("segm", 256), ("fabs", 256), ("fx", 528), ("m33", 528), ("oha", 2048), ("ohf", 256), ("eq", 2048)],
 }
 ALIAS = {}
 for (_b, _d), _l in PARTS.items():
@@ -38,17 +35,21 @@ for (_b, _d), _l in PARTS.items():
         ALIAS[_n] = (_b, _o, _w)
         _o += _w
     SCRATCH[_b] = ("sbuf", [128, _o], _d)
-SEMAPHORES = ["V", "S", "T", "G", "key", "x", "st", "hist", "map", "dat", "loc", "tx", "tl", "tw"] + ["hop%d" % _i for _i in range(len(RELAYW))]
+NIN = 4
+SEMAPHORES = (["V", "S", "T", "G", "key", "st", "hist", "map", "dat", "loc", "tx0", "tx1"] + ["x%d" % _i for _i in range(len(PIECES))]
+              + [_s + "%d" % _i for _s in ("in", "mi", "late") for _i in range(NIN)])
 
 
 def rank_program(g, core, T, topo):
     r = T.rank_of(core)
     neng = lambda m: bin(m).count("1")
     near = lambda a, b: topo.chip(T.cores[a]) == topo.chip(T.cores[b])
+    rot = lambda q: [(q + k) % N for k in range(1, N)]
+    farof = lambda q: [d for d in rot(q) if not near(q, d)]
+    sibof = lambda q: [d for d in rot(q) if near(q, d)]
 
-    def order(q):
-        rot = [(q + k) % N for k in range(1, N)]
-        return [d for d in rot if not near(q, d)] + [d for d in rot if near(q, d)]
+    def samedie(q):
+        return [d for d in farof(q) if topo.die(T.cores[d]) == topo.die(T.cores[q])]
 
     last = topo.chip(max(T.cores))
     ncore = max(T.cores) + 1
@@ -56,14 +57,89 @@ def rank_program(g, core, T, topo):
         ncore += 1
 
     def relay(q, k):
-        c = T.cores[order(q)[k]]
-        own = [h for h in range(ncore) if topo.mates(topo.chip(h), topo.chip(c)) and topo.die(h) == topo.die(T.cores[q]) and topo.may_write(h, c)]
-        return own[RELAYW.index(k) % len(own)]
+        c = T.cores[samedie(q)[k]]
+        own = [h for h in range(ncore) if topo.mates(topo.chip(h), topo.chip(c)) and topo.die(h) == topo.die(c) and topo.may_write(h, c)]
+        return own[k % len(own)]
 
-    def twin(q):
-        c, p = T.cores[q], relay(q, RELAYW[0])
-        return [h for h in range(ncore) if topo.chip(h) == topo.chip(c) and topo.die(h) == topo.die(c) and T.rank_of(h) is None
-                and topo.may_write(h, p)][0]
+    def helpers(q):
+        c, p = T.cores[q], relay(q, 0)
+        free = [h for h in range(ncore) if topo.chip(h) == topo.chip(c) and topo.die(h) == topo.die(c) and T.rank_of(h) is None]
+        mate = [h for h in free if topo.may_write(h, p)][0]
+        return [h for h in free if h != mate][:2] + [mate]
+
+    def piece(q, i, cut=PIECES):
+        lo, hi = cut[i]
+        return T.ld[:, NT * q + lo:NT * q + hi]
+
+    nloc = [0]
+
+    def write(out, in_, sem, to, m):
+        rid, pid, _ = topo.addr(to)
+        g.remote_dma(out, in_, T.sem[sem], T.sem.loc, pid, rid, m)
+        nloc[0] += neng(m)
+
+    def dst(d):
+        rid, pid, _ = topo.addr(T.cores[d])
+        return DstId(rid=rid, pnc=pid)
+
+    def both(p, d, m):
+        ds = [d] + sibof(d)
+        g.remote_dma_fused([RemoteDMATransfer(dst_ids=[dst(e) for e in ds], dma_engine_mask=m, remote_sem=T.sem.dat,
+                                              srcs=[p], dsts=[p] * len(ds))], local_sem=T.sem.loc)
+        nloc[0] += neng(m)
+
+    def masks(q):
+        off = topo.mask(T.cores[q], T.cores[farof(q)[0]])
+        full = topo.mask(T.cores[q], T.cores[sibof(q)[0]])
+        return off, full & ~off, full
+
+    def handm(q, i):
+        off, nr, full = masks(q)
+        ks = range(len(samedie(q)))
+        todo = [(3 * k + 5, "mi", k, (i, SUBS)) for k in ks]
+        if i in WHO[EARLY:]:
+            todo += [(k, "in", k, (WHO.index(i), PIECES)) for k in ks]
+            todo += [(3 * k + 6, "late", k, (EARLY + WHO[EARLY:].index(i), PIECES)) for k in ks]
+        todo.sort(key=lambda e: e[0])
+        return [(sem, k, at, full if 4 * n >= 3 * len(todo) else nr) for n, (_, sem, k, at) in enumerate(todo)]
+
+    if r is None:
+        for q in range(N):
+            hq = helpers(q)
+            if core not in hq:
+                continue
+            i = hq.index(core)
+            offm, nearm, full = masks(q)
+
+            def handon(early):
+                for sem, k, (p, cut), m in handm(q, i):
+                    if (sem == "in") == early:
+                        src = [s for s in samedie(q) if samedie(s)[k] == q][0]
+                        g.wait_ge(T.sem["%s%d" % (sem, k)], neng(offm))
+                        both(piece(src, p, cut), q, m)
+
+            for p in range(len(PIECES)):
+                if WHO[p] != i:
+                    continue
+                late = p >= EARLY
+                g.wait_ge(T.sem["tx%d" % late], neng(nearm if late else full))
+                for k, d in enumerate(samedie(q)):
+                    to = relay(q, k) if i == 2 else helpers(d)[i]
+                    write(piece(q, p), piece(q, p), ("late%d" if late else "in%d") % k, to, topo.mask(core, to))
+                if not late:
+                    handon(True)
+            handon(False)
+        for k in range(NIN):
+            for q in range(N):
+                if relay(q, k) == core:
+                    d = samedie(q)[k]
+                    g.wait_ge(T.sem["in%d" % k], neng(topo.mask(helpers(q)[2], core)))
+                    for i in (2, 0, 1):
+                        to = helpers(d)[i]
+                        write(piece(q, i, SUBS), piece(q, i, SUBS), "mi%d" % k, to, topo.mask(core, to))
+        if nloc[0]:
+            g.wait_ge(T.sem.loc, nloc[0])
+        return
 
     eng = {"V": g.vector, "S": g.scalar, "T": g.tensor, "G": g, "Y": g.sync}
     log, seen, cnt = {}, {}, {}
@@ -131,10 +207,8 @@ def rank_program(g, core, T, topo):
         else:
             do("S", lambda: g.scalar.activation(o[0], i[0], func, bias=b, scale=s, accum_out=acc[0]), [o, acc], [i] + cols)
 
-    def scan(o, d0, d1, init):
-        s = [init] if isinstance(init, tuple) else []
-        v = init[0] if isinstance(init, tuple) else init
-        do("V", lambda: g.vector.tensor_tensor_scan(o[0], d0[0], d1[0], v, Op.mult, Op.add), [o], [d0, d1] + s)
+    def addmult(o, d0, d1):
+        do("V", lambda: g.vector.tensor_tensor_scan(o[0], d0[0], d1[0], 0.0, Op.add, Op.mult), [o], [d0, d1])
 
     def mm(o, l, rh, start=True, stop=True):
         do("T", lambda: g.tensor.matmul(o[0], l[0], rh[0], start, stop), [o], [l, rh])
@@ -148,301 +222,197 @@ def rank_program(g, core, T, topo):
         else:
             do(q, lambda: g.scalar.activation(o[0], win[0].indirect(off[0]), Act.Copy), [o], [win, off])
 
-    bcol = lambda d: A("scb", 16 * d + 15, 16 * d + 16)
-    wslot = lambda d: A("wnd", CAP * d, CAP * d + CAP)
-    nloc = [0]
-
-    def groupcols():
-        ts(A("pbit", 0, 1), A("pint"), 15, Op.bitwise_and)
-        ts(A("pbit", 1, 2), A("pint"), 4, Op.arith_shift_right)
-        cp(A("pdig"), A("pbit"))
-        ts(A("io32"), A("io32"), A("pdig", 0, 1), Op.add)
-
-    def offsets(d):
-        ts(A("wl", 32 * d, 32 * d + 32), A("io32"), bcol(d), Op.add, NT - 1.0, Op.min)
-
-    def window(q, d, o):
-        gather(q, o, A("xs"), A("wl", 32 * d, 32 * d + 32))
-
-    def write(out, in_, sem, to, m):
-        rid, pid, _ = topo.addr(to)
-        g.remote_dma(out, in_, T.sem[sem], T.sem.loc, pid, rid, m)
-        nloc[0] += neng(m)
-
-    def send(q, d, m, src=None):
-        guard("G", [], [wslot(d)] if src is None else [])
-        write(T.ld[:, CAP * q:CAP * q + CAP], wslot(d)[0] if src is None else src, "dat", T.cores[d], m)
-
-    passed = lambda i: T.wnd[:, CAP * i:CAP * i + CAP]
-    if r is None:
-        for q in range(N):
-            if twin(q) != core:
-                continue
-            ds = [order(q)[k] for k in TWINW]
-            nm = neng(topo.mask(T.cores[q], core) & ~topo.mask(T.cores[q], T.cores[ds[0]]))
-            for sem, buf in (("tx", "xb"), ("tl", "slist"), ("tw", "scb")):
-                note(sem, nm, sem, [A(buf)], [])
-            iota(A("pint"), [[0, 1]], 0, 1)
-            iota(A("io32"), [[16, 32]], 0, 0)
-            groupcols()
-            gather("S", A("xs", 0, 1024), A("xb"), A("slist", 0, 64))
-            gather("V", A("xs", 1024, 2048), A("xb"), A("slist", 64, 128))
-            for d in ds:
-                offsets(d)
-            for n, (k, d) in enumerate(zip(TWINW, ds)):
-                window("VS"[n % 2], d, wslot(d))
-                if k in RELAYW:
-                    i, h = RELAYW.index(k), relay(q, k)
-                    guard("G", [], [wslot(d)])
-                    write(passed(i), wslot(d)[0], "hop%d" % i, h, topo.mask(core, h))
-                else:
-                    send(q, d, topo.mask(core, T.cores[d]))
-            for sem, c in (("V", cnt["V"]), ("S", cnt["S"]), ("G", cnt["G"]), ("tx", nm), ("tl", nm), ("tw", nm)):
-                g.wait_ge(T.sem[sem], c)
-        for i, k in enumerate(RELAYW):
-            for q in range(N):
-                if relay(q, k) == core:
-                    d = order(q)[k]
-                    g.wait_ge(T.sem["hop%d" % i], neng(topo.mask(twin(q), core)))
-                    send(q, d, topo.mask(core, T.cores[d]), passed(i))
-        if nloc[0]:
-            g.wait_ge(T.sem.loc, nloc[0])
-        return
-
-    peers = order(r)
-    sibs = [d for d in peers if near(r, d)]
-    far = [d for d in peers if not near(r, d)]
-    offm = topo.mask(core, T.cores[far[0]])
-    nearm = topo.mask(core, T.cores[sibs[0]]) & ~offm
+    peers, far, sibs = farof(r) + sibof(r), farof(r), sibof(r)
+    offm, nearm, full = masks(r)
     offbits = [1 << i for i in range(16) if offm >> i & 1]
-
-    def dst(d):
-        rid, pid, _ = topo.addr(T.cores[d])
-        return DstId(rid=rid, pnc=pid)
-
-    def share(buf, sem):
-        guard("G", [], [A(buf)])
-        write(T[buf][:], T[buf][:], sem, twin(r), nearm)
 
     g.sync.dma_start(T.key16[:], T.key[:]).then_inc(T.sem.key, 16)
     note("key", 16, "dkey", [A("key16")], [])
-    g.sync.dma_start(T.xb[:], T.x[:]).then_inc(T.sem.x, 16)
-    note("x", 16, "dx", [A("xb")], [])
+    for i in FIRST:
+        lo, hi = PIECES[i]
+        g.sync.dma_start(piece(r, i), T.x[:, lo:hi]).then_inc(T.sem["x%d" % i], 16)
+        note("x%d" % i, 16, "dx", [A("ld", NT * r + lo, NT * r + hi)], [])
 
     iota(A("pcol"), [[0, 1]], 0, 1)
     iota(A("iow"), [[1, 160]], 0, 0)
+    iota(A("cm16"), [[1, 16]], -15, 0)
+    iota(A("jv1"), [[128, 16]], 1, 1)
+    iota(A("c33"), [[1, 17], [0, 2]], -16, 0)
     iota(A("io16"), [[0, 16], [1, 16]], 0, 0)
-    iota(A("jv"), [[128, 16]], 0, 1)
     iota(A("pint"), [[0, 1]], 0, 1)
-    iota(A("io32"), [[16, 32]], 0, 0)
-    fill(A("ones"), 1.0)
-    fill(A("ph", 0, 1), 0.0)
-    ts(A("z16"), A("ones", 0, 240, p=16), 0.0, Op.mult)
-    ts(A("hp", 0, 1), A("ones", 0, 1), 0.0, Op.mult)
-    cp(A("onesf"), A("ones", 0, 128))
-    ts(A("abias"), A("pcol"), -16.0, Op.mult, -7.5, Op.add)
     w128 = A("iow", 0, 128)
+    fill(A("ones"), 1.0)
+    fill(A("zz"), 0.0)
+    fill(A("ph", 0, 1), 0.0)
+    ts(A("z16"), A("zz", 0, 240, p=16), 0.0, Op.mult)
+    ts(A("idf"), A("iow", 0, 16, p=16), A("pcol", p=16), Op.is_equal)
+    ts(A("z16", 112, 128), A("iow", 0, 16, p=16), A("pcol", p=16), Op.is_equal, after=[A("z16", 112, 128)])
     ts(A("ident"), w128, A("pcol"), Op.is_equal)
     for q in range(4):
         ts(A("pen", 128 * q, 128 * q + 128), w128, A("pcol"), Op.is_le, 0.25, Op.mult)
+    ts(A("i16"), w128, 16.0, Op.mult)
+    ts(A("abias"), A("pcol"), -16.0, Op.mult, -7.5, Op.add)
+    for b in range(16):
+        act(A("rowsel", 128 * b, 128 * b + 128), A("ones", 0, 128, p=16), Act.Copy, scale=A("idf", b, b + 1))
     for q in range(2):
         mm(A("kb%d" % q), A("ident"), A("pen"), True, False)
-    ts(A("idf"), A("iow", 0, 16, p=16), A("pcol", p=16), Op.is_equal)
-    ts(A("z16", 112, 128), A("iow", 0, 16, p=16), A("pcol", p=16), Op.is_equal, after=[A("z16", 112, 128)])
-    for b in range(16):
-        o = A("rowsel", 128 * b, 128 * b + 128)
-        if b % 2 or b > 8:
-            act(o, A("ones", 0, 128, p=16), Act.Copy, scale=A("idf", b, b + 1))
-        else:
-            ts(o, A("ones", 0, 128, p=16), A("idf", b, b + 1), Op.mult)
-    cp(A("kd", 0, 128), A("key16"))
-    ts(A("kint", 0, 128), A("key16"), 4, Op.arith_shift_right)
-    ts(A("kint", 128, 256), A("key16"), 15, Op.bitwise_and)
+    ts(A("segm"), A("io16"), 0.0, Op.is_gt)
+    ts(A("loc", 256, 272), A("ones", 0, 16), 0.0, Op.mult)
+    ts(A("tab", 0, 1), A("ones", 0, 1), 0.0, Op.mult)
+
+    def setout(ps):
+        for p in ps:
+            guard("G", [], [A("ld", NT * r + PIECES[p][0], NT * r + PIECES[p][1])])
+            write(piece(r, p), piece(r, p), "tx%d" % (p >= EARLY), helpers(r)[WHO[p]], nearm if p >= EARLY else full)
+
+    setout(FIRST[:EARLY])
+    cp(A("kd"), A("key16"))
+    for c in range(8):
+        mm(A("pt", 0, 16), A("z16", 112 - 16 * c, 240 - 16 * c), A("kd", c, 128, 8), c == 0, c == 7)
     for c in range(8):
         mm(A("pk", 64 + 16 * c, 80 + 16 * c, p=16), A("kd", c, 128, 8), A("z16", 112, 128))
-    cp(A("kd", 128, 256), A("kint", 0, 128))
-    ts(A("kd", 256, 384), A("kint", 128, 256), -1.0, Op.mult)
-    for c in range(8):
-        mm(A("pt", 0, 48), A("z16", 112 - 16 * c, 240 - 16 * c), A("kd", c, 384, 8), c == 0, c == 7)
+    mm(A("kb2"), A("ident"), A("pen"), True, False)
+    cp(A("ktd"), A("pt", 0, 16))
+    ts(A("adivi"), A("ktd"), 1.0 / 16, Op.mult, -0.5 + 0.5 / 16, Op.add)
+    ts(A("a16"), A("adivi"), 16.0, Op.mult)
+    tt(A("u"), A("a16"), A("ktd"), Op.subtract)
     act(A("ktt"), A("pk", 64, 192, p=16), Act.Copy)
-    cp(A("ktd"), A("pt", 0, 48))
 
     def keyrows(q):
-        if q > 1:
-            mm(A("kb%d" % q), A("ident"), A("pen"), True, False)
         for b in range(4 * q, 4 * q + 4):
             mm(A("kb%d" % q, 128 * (b % 4), 128 * (b % 4) + 128), A("rowsel", 128 * b, 128 * b + 128), A("ktt"), False, b % 4 == 3)
 
     def absrow(q):
         act(A("kabs", 512 * q, 512 * q + 512), A("kb%d" % q), Act.Abs, bias=A("abias"))
 
-    def digitrow(lo, hi):
-        ts(A("oht", lo, hi), A("kabs", lo, hi), 8.0, Op.is_lt)
+    def digitrow(q):
+        ts(A("oht", 512 * q, 512 * q + 512), A("kabs", 512 * q, 512 * q + 512), 8.0, Op.is_lt)
 
     def equal(q):
         for b in range(4 * q, 4 * q + 4):
             ts(A("eq", 128 * b, 128 * b + 128), A("kb%d" % q, 128 * (b % 4), 128 * (b % 4) + 128), A("ktd", b, b + 1), Op.is_equal)
 
-    for b in range(8):
-        act(A("fabs", 16 * b, 16 * b + 16), A("iow", 0, 16), Act.Abs, bias=A("ktd", 32 + b, 33 + b))
-    act(A("ohf", 0, 128), A("fabs", 0, 128), Act.Relu, bias=A("ones", 0, 1), scale=-1.0)
+    SB = 10
+    for b in range(SB):
+        act(A("fabs", 16 * b, 16 * b + 16), A("cm16"), Act.Abs, bias=A("u", b, b + 1), scale=-1.0)
+    act(A("ohf", 0, 16 * SB), A("fabs", 0, 16 * SB), Act.Relu, bias=A("ones", 0, 1), scale=-1.0)
     for b in range(16):
-        ts(A("oha", 128 * b, 128 * b + 128), w128, A("ktd", 16 + b, 17 + b), Op.is_equal)
-    for b in range(8, 16):
-        ts(A("ohf", 16 * b, 16 * b + 16), A("iow", 0, 16), A("ktd", 32 + b, 33 + b), Op.add, 0.0, Op.is_equal)
+        ts(A("oha", 128 * b, 128 * b + 128), A("i16"), A("a16", b, b + 1), Op.is_equal)
+    for b in range(SB, 16):
+        ts(A("ohf", 16 * b, 16 * b + 16), A("cm16"), A("u", b, b + 1), Op.is_equal)
     keyrows(0)
     keyrows(1)
     for b in range(16):
         mm(A("ph", 1 + b, 242 + b, 16), A("oha", 128 * b, 128 * b + 128), A("ohf", 16 * b, 16 * b + 16))
     absrow(0)
-    equal(0)
-    ts(A("lst"), w128, A("pcol"), Op.is_gt)
-    scan(A("scan0"), A("ones", 0, 257), A("ph", 0, 257), 0.0)
-    tt(A("hs"), A("scan0", 16, 257, 16), A("scan0", 0, 241, 16), Op.subtract)
+    absrow(1)
+    addmult(A("loc", 0, 256), A("ph", 0, 256), A("segm"))
+    tt(A("hs"), A("loc", 15, 256, 16), A("ph", 16, 257, 16), Op.add)
     guard("G", [], [A("hs")])
-    for ds, m in ((far, offm), (sibs, nearm)):
-        g.remote_dma_fused([RemoteDMATransfer(dst_ids=[dst(d) for d in ds], dma_engine_mask=m, remote_sem=T.sem.hist, srcs=[T.hs[:]],
-                                              dsts=[T.hl[:, 16 * r:16 * r + 16]] * len(ds))], local_sem=T.sem.loc)
-        nloc[0] += neng(m)
-    nhist = neng(offm) * len(far) + neng(nearm) * len(sibs)
+    g.remote_dma_fused([RemoteDMATransfer(dst_ids=[dst(d) for d in peers], dma_engine_mask=offm, remote_sem=T.sem.hist, srcs=[T.hs[:]],
+                                          dsts=[T.hl[:, 16 * r:16 * r + 16]] * len(peers))], local_sem=T.sem.loc)
+    nloc[0] += neng(offm)
+    nhist = neng(offm) * len(peers)
+    setout(FIRST[EARLY:])
+    for d in sibs:
+        mine = T.ld[:, NT * r:NT * r + NT]
+        write(mine, mine, "dat", T.cores[d], nearm)
     for d in peers:
         note("hist", nhist, "rh", [A("hl", 16 * d, 16 * d + 16)], [])
-    share("xb", "tx")
+    mm(A("kb3"), A("ident"), A("pen"), True, False)
     keyrows(2)
-    mm(A("pk", 0, 1), A("lst"), A("scan0", 256, 257))
     keyrows(3)
-    absrow(1)
-    equal(1)
-    digitrow(0, 1024)
-    ts(A("tbl"), A("scan0", 0, 256), A("pk", 0, 1), Op.add)
-    absrow(2)
-    equal(2)
-    groupcols()
-    for d in range(N):
-        act(A("hrep", 16 * d, 16 * d + 16), A("hs"), Act.Copy)
     cp(A("hl", 16 * r, 16 * r + 16), A("hs"))
-    digitrow(1024, 1536)
-    ts(A("segm"), A("io16"), 0.0, Op.is_gt)
+    equal(0)
+    digitrow(0)
+    equal(1)
+    digitrow(1)
+    tt(A("ltab"), A("loc", 0, 256), A("loc", 16, 272), Op.subtract)
+    absrow(2)
     absrow(3)
-    digitrow(1536, 2048)
+    for b in range(16):
+        act(A("fx", 33 * b, 33 * b + 33), A("c33", 1, 34), Act.Relu, bias=A("u", b, b + 1), scale=-1.0)
+    act(A("m33"), A("fx"), Act.Relu, bias=A("ones", 0, 1), scale=-1.0)
+    equal(2)
+    digitrow(2)
     equal(3)
-    half = lambda h: A("pl" if h == 0 else "ph", 0, 128)
-
-    def lookup(h):
-        for b in range(8 * h, 8 * h + 8):
-            o = A("pl" if h == 0 else "ph", 16 * (b % 8), 16 * (b % 8) + 16)
-            mm(o, A("oht", 128 * b, 128 * b + 128), A("tbl", b, 241 + b, 16))
-
-    def count(lo, hi):
-        for b in range(lo, hi):
-            mm(A("pt", 256 + b, 257 + b), A("eq", 128 * b, 128 * b + 128), A("ones", 0, 1))
-
-    def pick(prod, out, h):
-        tt(A(prod, 128 * h, 128 * h + 128), half(h), A("ohf", 128 * h, 128 * h + 128), Op.mult)
-        scan(A(out, 128 * h, 128 * h + 128), A("segm", 0, 128), A(prod, 128 * h, 128 * h + 128), 0.0)
-
-    lookup(0)
-    count(0, 12)
-    lookup(1)
-    count(12, 16)
-    pick("prod", "scan", 0)
-    pick("prod", "scan", 1)
-    tt(A("lr"), A("scan", 15, 256, 16), A("pt", 256, 272), Op.add)
-
-    def digits(v, bits, di, df, mu, mo):
-        n = float(1 << bits)
-        ts(A(di), A(v), 1.0 / n, Op.mult, -0.5 + 0.5 / n, Op.add)
-        ts(A(mu), A(di), n, Op.mult)
-        cp(A(df), A(di))
-        tt(A(mo), A(v), A(mu), Op.subtract)
-
-    digits("lr", 4, "divi", "divf", "dmul", "modf")
+    digitrow(3)
+    ts(A("lst"), w128, A("pcol"), Op.is_gt)
+    ts(A("iowk"), A("iow"), 128.0, Op.mult)
+    ts(A("jvn"), A("jv1"), -1.0 / 128, Op.mult)
+    acc = lambda b, lo=0, hi=33, step=1: A("pl" if b < 8 else "pt", 33 * (b % 8) + lo, 33 * (b % 8) + hi, step)
+    ohb = lambda name, b: A(name, 128 * b, 128 * b + 128)
+    for p in ("pl", "pt"):
+        mm(A(p, 0, 264), A("ident"), A("zz"), True, False)
+    mm(A("pk", 0, 16), A("ident"), A("zz", 0, 16), True, False)
     for b in range(16):
-        o = 128 * b
-        ts(A("sl", o, o + 128), A("io16", 0, 128), A("modf", b, b + 1), Op.is_equal)
-        ts(A("sr", o, o + 128), w128, A("divf", b, b + 1), Op.is_equal, A("jv", b, b + 1), Op.mult)
-        mm(A("pt", 0, 128), A("sl", o, o + 128), A("sr", o, o + 128), b == 0, b == 15)
-    cp(A("slist"), A("pt", 0, 128))
-    share("slist", "tl")
-    act(A("junk"), A("hl"), Act.Copy, scale=-1.0, acc=A("rowt", 1, 2))
+        mm(acc(b, 1, 33, 2), ohb("oht", b), A("ltab", b, 241 + b, 16), False, False)
+        mm(acc(b, 32, 33), ohb("eq", b), A("ones", 0, 1), False, False)
+    act(A("junk"), A("hl"), Act.Copy, acc=A("rowt"))
     for d in range(N):
-        act(A("hp", 1 + d, 152 + d, 10), A("hl", 16 * d, 16 * d + 16), Act.Copy, scale=-1.0)
-    gather("S", A("xs"), A("xb"), A("slist"))
-    mm(A("pk", 1, 2), A("lst"), A("rowt", 1, 2))
-    scan(A("base"), A("ones", 0, 160), A("hp", 0, 160), A("pk", 1, 2))
-    own = A("base", r, 151 + r, 10)
-    tt(A("dt"), own, A("tbl", 0, 241, 16), Op.add)
-    cp(A("dh"), A("dt"))
-    tt(A("dl"), A("dt"), A("dh"), Op.subtract)
-
-    def places(h):
-        for b in range(8 * h, 8 * h + 8):
-            o = A("pl" if h == 0 else "ph", 16 * (b % 8), 16 * (b % 8) + 16)
-            mm(o, A("oht", 128 * b, 128 * b + 128), A("dh"), True, False)
-            mm(o, A("oht", 128 * b, 128 * b + 128), A("dl"), False, True)
-
-    places(0)
-    for d in range(N):
-        ts(A("xr", 16 * d, 16 * d + 16), own, 2048.0 * d, Op.add, 0.0, Op.max)
-    tt(A("xm"), A("xr"), A("hrep"), Op.min)
-    ts(A("lr1"), A("lr"), 1.0, Op.add)
-    pick("prod2", "scan2", 0)
-    mm(A("pk", 16, 176), A("onesf"), A("xm"))
-    places(1)
-    scan(A("scb"), A("segm", 0, 160), A("pk", 16, 176), 0.0)
-    share("scb", "tw")
-    mine = [peers[k] for k in MAINW]
-    for d in mine + [r]:
-        offsets(d)
-    for d in mine:
-        window("S", d, wslot(d))
-        if d in far:
-            send(r, d, offm)
-    window("S", r, A("ld", CAP * r, CAP * r + CAP))
-    pick("prod2", "scan2", 1)
-    tt(A("pos"), A("lr"), A("scan2", 15, 256, 16), Op.subtract)
-    digits("pos", 7, "pdivi", "pdivf", "pmul", "pmod")
+        if d < r:
+            mm(A("pk", 0, 16), A("ident"), A("hl", 16 * d, 16 * d + 16), False, False)
+        else:
+            mm(A("pk", 0, 15), A("ident"), A("hl", 16 * d + 1, 16 * d + 16), False, False)
+    mm(A("pk", 15, 16), A("lst"), A("rowt"), False, True)
+    cp(A("tab", 1, 33, 2), A("pk", 0, 16))
+    tt(A("tab", 2, 33, 2), A("pk", 0, 16), A("tab", 1, 33, 2), Op.subtract)
     for b in range(16):
-        ts(A("ml", 128 * b, 128 * b + 128), w128, A("pmod", b, b + 1), Op.is_equal)
-        ts(A("mr", 160 * b, 160 * b + 160), A("iow", 0, 160), A("pdivf", b, b + 1), Op.is_equal, A("lr1", b, b + 1), Op.mult)
-        mm(A("kb0", 0, 160), A("ml", 128 * b, 128 * b + 128), A("mr", 160 * b, 160 * b + 160), b == 0, b == 15)
-    mt = lambda ap: (ap, "mt", 0, 320)
-    for d in range(N):
-        ts(mt(T.mt[:, d, 0:16]), A("kb0", 16 * d, 16 * d + 16), bcol(d), Op.subtract, 0.0, Op.max)
-    ts(mt(T.mt[:, :, 16:32]), mt(T.mt[:, :, 0:16]), 0.0, Op.is_gt, float(CAP * r), Op.mult)
-    guard("G", [], [mt(None)])
+        mm(acc(b), ohb("oht", b), A("tab"), False, b % 8 == 7)
+    for h in range(2):
+        lo = 264 * h
+        addmult(A("scan", lo, lo + 264), A("pl" if h == 0 else "pt", 0, 264), A("m33", lo, lo + 264))
+        pos = lambda a, b: A("scan", 33 * a + 32, 33 * (b - 1) + 33, 33)
+        ts(A("pdivi", 8 * h, 8 * h + 8), pos(8 * h, 8 * h + 8), 1.0 / 128, Op.mult, -0.5 + 0.5 / 128, Op.add)
+        ts(A("pmul", 8 * h, 8 * h + 8), A("pdivi", 8 * h, 8 * h + 8), 128.0, Op.mult)
+        for b in range(8 * h, 8 * h + 8):
+            ts(ohb("ml", b), w128, A("pmul", b, b + 1), Op.add, pos(b, b + 1), Op.is_equal)
+            m = A("mr", 160 * b, 160 * b + 160)
+            if b % 8 in (3, 5, 7):
+                x = A("mx", 160 * b, 160 * b + 160)
+                act(x, A("iowk"), Act.Abs, bias=A("pmul", b, b + 1), scale=-1.0)
+                act(m, x, Act.Relu, bias=A("jv1", b, b + 1), scale=A("jvn", b, b + 1))
+            else:
+                ts(m, A("iowk"), A("pmul", b, b + 1), Op.is_equal, A("jv1", b, b + 1), Op.mult)
+            mm(A("kb0", 0, 160), ohb("ml", b), m, b == 0, b == 15)
+    ts(A("msk"), A("kb0", 0, 160), 0.0, Op.is_gt, float(NT * r), Op.mult)
+    tt(A("mt"), A("kb0", 0, 160), A("msk"), Op.add)
+    guard("G", [], [A("mt")])
     nmap = len(far) + neng(nearm) * len(sibs)
     tr = []
     for d in peers:
         m = nearm if d in sibs else offbits[far.index(d) % len(offbits)]
         tr.append(RemoteDMATransfer(dst_ids=[dst(d)], dma_engine_mask=m, remote_sem=T.sem.map,
-                                    srcs=[T.mt[:, d, 0:32]], dsts=[T.lm[:, 32 * r:32 * r + 32]]))
+                                    srcs=[T.mt[:, 16 * d:16 * d + 16]], dsts=[T.lm[:, 16 * r:16 * r + 16]]))
         nloc[0] += neng(m)
-        note("map", nmap, "rm", [A("lm", 32 * d, 32 * d + 32)], [])
+        note("map", nmap, "rm", [A("lm", 16 * d, 16 * d + 16)], [])
     g.remote_dma_fused(tr, local_sem=T.sem.loc)
-    cp(A("lm", 32 * r, 32 * r + 32), mt(T.mt[:, r, 0:32]))
-    for d in sibs:
-        send(r, d, nearm)
+    cp(A("lm", 16 * r, 16 * r + 16), A("mt", 16 * r, 16 * r + 16))
+    ts(A("pbit", 0, 1), A("pint"), 15, Op.bitwise_and)
+    ts(A("pbit", 1, 2), A("pint"), 4, Op.arith_shift_right)
+    cp(A("pdig"), A("pbit"))
     ts(A("wrap"), A("io16", 0, 128), A("pdig", 0, 1), Op.is_equal)
     ts(A("m8"), A("iow", 0, 8), A("pdig", 1, 2), Op.is_equal)
     for c in range(8):
         ts(A("rl", 128 * c, 128 * c + 128), A("wrap"), A("m8", c, c + 1), Op.mult)
-    got = neng(offm) * len(far) + neng(nearm) * len(sibs)
+    got = neng(nearm) * len(sibs) + sum(neng(m) for q in [r] + sibs for i in range(3) for _, _, _, m in handm(q, i))
     for d in peers:
-        note("dat", got, "rd", [A("ld", CAP * d, CAP * d + CAP)], [])
-    tt(A("t1"), A("lm", 0, 160), A("lm", 160, 320), Op.add)
-    tt(A("t2"), A("t1", 0, 64), A("t1", 64, 128), Op.add)
-    tt(A("t3"), A("t2", 0, 32), A("t2", 32, 64), Op.add)
-    tt(A("t4"), A("t3"), A("t1", 128, 160), Op.add)
+        note("dat", got, "rd", [A("ld", NT * d, NT * d + NT)], [])
+    tt(A("t1"), A("lm", 0, 80), A("lm", 80, 160), Op.add)
+    tt(A("t2"), A("t1", 0, 32), A("t1", 32, 64), Op.add)
+    tt(A("t3"), A("t2", 0, 16), A("t2", 16, 32), Op.add)
+    tt(A("t4"), A("t3"), A("t1", 64, 80), Op.add)
+    cp(A("th"), A("t4"))
+    tt(A("tl"), A("t4"), A("th"), Op.subtract)
     for c in range(8):
         o = A("kb1", c, 121 + c, 8)
-        mm(o, A("rl", 128 * c, 128 * c + 128), A("t4", 0, 16), True, False)
-        mm(o, A("rl", 128 * c, 128 * c + 128), A("t4", 16, 32), False, True)
+        mm(o, A("rl", 128 * c, 128 * c + 128), A("th"), True, False)
+        mm(o, A("rl", 128 * c, 128 * c + 128), A("tl"), False, True)
     ts(A("flist"), A("kb1", 0, 128), -1.0, Op.add)
     for n, (lo, hi) in enumerate(zip(PARTY, PARTY[1:])):
         gather("VS"[n % 2], A("yb", lo, hi), A("ld"), A("flist", lo // 16, hi // 16))
         guard("Y", [], [A("yb", lo, hi)])
         g.sync.dma_start(T.y[:, lo:hi], T.yb[:, lo:hi]).then_inc(T.sem.st, 16)
-    for sem, c in [(q, cnt[q]) for q in "VSTG"] + [("key", 16), ("x", 16), ("loc", nloc[0]), ("hist", nhist), ("map", nmap), ("dat", got),
-                                                   ("st", 16 * (len(PARTY) - 1))]:
+    for sem, c in ([(q, cnt[q]) for q in "VSTG"] + [("key", 16)] + [("x%d" % i, 16) for i in FIRST]
+                   + [("loc", nloc[0]), ("hist", nhist), ("map", nmap), ("dat", got), ("st", 16 * (len(PARTY) - 1))]):
         g.wait_ge(T.sem[sem], c)

from concourse.bass import DstId, RemoteDMATransfer
from concourse.mybir import AluOpType as Op, ActivationFunctionType as Act

B16, F16, F32, I32, U16 = "bfloat16", "float16", "float32", "int32", "uint16"
N, NT = 10, 2048
PIECES = ((0, 144), (144, 288), (288, 1184), (1184, 1616), (1616, 2048))
WHO = (0, 1, 2, 0, 1)
EARLY = 3
FIRST = (2, 0, 1, 3, 4)
SUBS = ((288, 512), (512, 736), (736, 1184))
PARTY = (0, 512, 1024, 1312, 1600, 1824, 2048)
SCRATCH = {
    "idf": ("sbuf", [16, 16], F32), "rowsel": ("sbuf", [16, 2048], F16), "z16": ("sbuf", [16, 240], F16),
    "key16": ("sbuf", [16, 128], I32), "kd": ("sbuf", [16, 128], F16), "ktt": ("sbuf", [16, 128], F16),
    "ml": ("sbuf", [128, 2048], F16), "mr": ("sbuf", [128, 2560], F16), "mx": ("sbuf", [128, 2560], F32),
    "mt": ("sbuf", [128, 160], F32), "lm": ("sbuf", [128, 160], F32),
    "hs": ("sbuf", [128, 16], F16), "hl": ("sbuf", [128, 160], F16), "flist": ("sbuf", [128, 128], U16),
    "ld": ("sbuf", [128, N * NT], B16), "yb": ("sbuf", [128, 2048], B16),
}
for _k in ("pk", "ph", "pt", "pl", "kb0", "kb1", "kb2", "kb3"):
    SCRATCH[_k] = ("psum", [128, 512], F32)
PARTS = {
    ("ff", F32): [("pcol", 1), ("pdig", 2), ("jv1", 16), ("jvn", 16), ("abias", 1), ("m8", 8), ("lst", 128), ("ktd", 16), ("a16", 16),
                  ("u", 16), ("rowt", 1), ("scan", 528), ("pmul", 16), ("msk", 160), ("t1", 80), ("t2", 32), ("t3", 16), ("t4", 16)],
    ("ii", I32): [("pint", 1), ("pbit", 2), ("adivi", 16), ("pdivi", 16)],
    ("hh", F16): [("ident", 128), ("pen", 512), ("rl", 1024), ("wrap", 128), ("kabs", 2048), ("oht", 2048), ("loc", 272),
                  ("ltab", 256), ("tab", 33), ("junk", 160), ("th", 16), ("tl", 16)],
    ("bb", B16): [("iow", 160), ("iowk", 160), ("i16", 128), ("io16", 256), ("cm16", 16), ("c33", 34), ("ones", 256), ("zz", 264),
                  ("segm", 256), ("fabs", 256), ("fx", 528), ("m33", 528), ("oha", 2048), ("ohf", 256), ("eq", 2048)],
}
ALIAS = {}
for (_b, _d), _l in PARTS.items():
    _o = 0
    for _n, _w in _l:
        ALIAS[_n] = (_b, _o, _w)
        _o += _w
    SCRATCH[_b] = ("sbuf", [128, _o], _d)
NIN = 4
SEMAPHORES = (["V", "S", "T", "G", "key", "st", "hist", "map", "dat", "loc", "tx0", "tx1"] + ["x%d" % _i for _i in range(len(PIECES))]
              + [_s + "%d" % _i for _s in ("in", "mi", "late") for _i in range(NIN)])


def rank_program(g, core, T, topo):
    r = T.rank_of(core)
    neng = lambda m: bin(m).count("1")
    near = lambda a, b: topo.chip(T.cores[a]) == topo.chip(T.cores[b])
    rot = lambda q: [(q + k) % N for k in range(1, N)]
    farof = lambda q: [d for d in rot(q) if not near(q, d)]
    sibof = lambda q: [d for d in rot(q) if near(q, d)]

    def samedie(q):
        return [d for d in farof(q) if topo.die(T.cores[d]) == topo.die(T.cores[q])]

    last = topo.chip(max(T.cores))
    ncore = max(T.cores) + 1
    while topo.chip(ncore) == last or topo.mates(topo.chip(ncore), last):
        ncore += 1

    def relay(q, k):
        c = T.cores[samedie(q)[k]]
        own = [h for h in range(ncore) if topo.mates(topo.chip(h), topo.chip(c)) and topo.die(h) == topo.die(c) and topo.may_write(h, c)]
        return own[k % len(own)]

    def helpers(q):
        c, p = T.cores[q], relay(q, 0)
        free = [h for h in range(ncore) if topo.chip(h) == topo.chip(c) and topo.die(h) == topo.die(c) and T.rank_of(h) is None]
        mate = [h for h in free if topo.may_write(h, p)][0]
        return [h for h in free if h != mate][:2] + [mate]

    def piece(q, i, cut=PIECES):
        lo, hi = cut[i]
        return T.ld[:, NT * q + lo:NT * q + hi]

    nloc = [0]

    def write(out, in_, sem, to, m):
        rid, pid, _ = topo.addr(to)
        g.remote_dma(out, in_, T.sem[sem], T.sem.loc, pid, rid, m)
        nloc[0] += neng(m)

    def dst(d):
        rid, pid, _ = topo.addr(T.cores[d])
        return DstId(rid=rid, pnc=pid)

    def both(p, d, m):
        ds = [d] + sibof(d)
        g.remote_dma_fused([RemoteDMATransfer(dst_ids=[dst(e) for e in ds], dma_engine_mask=m, remote_sem=T.sem.dat,
                                              srcs=[p], dsts=[p] * len(ds))], local_sem=T.sem.loc)
        nloc[0] += neng(m)

    def masks(q):
        off = topo.mask(T.cores[q], T.cores[farof(q)[0]])
        full = topo.mask(T.cores[q], T.cores[sibof(q)[0]])
        return off, full & ~off, full

    def handm(q, i):
        off, nr, full = masks(q)
        ks = range(len(samedie(q)))
        todo = [(3 * k + 5, "mi", k, (i, SUBS)) for k in ks]
        if i in WHO[EARLY:]:
            todo += [(k, "in", k, (WHO.index(i), PIECES)) for k in ks]
            todo += [(3 * k + 6, "late", k, (EARLY + WHO[EARLY:].index(i), PIECES)) for k in ks]
        todo.sort(key=lambda e: e[0])
        return [(sem, k, at, full if 4 * n >= 3 * len(todo) else nr) for n, (_, sem, k, at) in enumerate(todo)]

    if r is None:
        for q in range(N):
            hq = helpers(q)
            if core not in hq:
                continue
            i = hq.index(core)
            offm, nearm, full = masks(q)

            def handon(early):
                for sem, k, (p, cut), m in handm(q, i):
                    if (sem == "in") == early:
                        src = [s for s in samedie(q) if samedie(s)[k] == q][0]
                        g.wait_ge(T.sem["%s%d" % (sem, k)], neng(offm))
                        both(piece(src, p, cut), q, m)

            for p in range(len(PIECES)):
                if WHO[p] != i:
                    continue
                late = p >= EARLY
                g.wait_ge(T.sem["tx%d" % late], neng(nearm if late else full))
                for k, d in enumerate(samedie(q)):
                    to = relay(q, k) if i == 2 else helpers(d)[i]
                    write(piece(q, p), piece(q, p), ("late%d" if late else "in%d") % k, to, topo.mask(core, to))
                if not late:
                    handon(True)
            handon(False)
        for k in range(NIN):
            for q in range(N):
                if relay(q, k) == core:
                    d = samedie(q)[k]
                    g.wait_ge(T.sem["in%d" % k], neng(topo.mask(helpers(q)[2], core)))
                    for i in (2, 0, 1):
                        to = helpers(d)[i]
                        write(piece(q, i, SUBS), piece(q, i, SUBS), "mi%d" % k, to, topo.mask(core, to))
        if nloc[0]:
            g.wait_ge(T.sem.loc, nloc[0])
        return

    eng = {"V": g.vector, "S": g.scalar, "T": g.tensor, "G": g, "Y": g.sync}
    log, seen, cnt = {}, {}, {}

    def A(name, lo=0, hi=None, step=1, p=None):
        buf, off, w = ALIAS[name] if name in ALIAS else (name, 0, T[name].shape[1])
        t = T[buf]
        lo, hi = off + lo, off + (w if hi is None else hi)
        p = t.shape[0] if p is None else p
        return (t[0:p, lo:hi:step] if step > 1 else t[0:p, lo:hi]), buf, lo, hi

    def guard(q, outs, ins):
        want = {}
        for w, accs in ((True, outs), (False, ins)):
            for _, name, lo, hi in accs:
                bank = SCRATCH[name][0] == "psum"
                for sem, c, e, iw, l, h in log.get(name, []):
                    meet = l < hi and lo < h
                    if e == q:
                        hit = meet and iw and not w
                    else:
                        hit = bank or (meet and (iw or w))
                    if hit:
                        want[sem] = max(want.get(sem, 0), c)
        for sem, c in want.items():
            if seen.get((q, sem), 0) < c:
                eng[q].wait_ge(T.sem[sem], c)
                seen[(q, sem)] = c

    def note(sem, c, e, outs, ins):
        for w, accs in ((True, outs), (False, ins)):
            for _, name, lo, hi in accs:
                log.setdefault(name, []).append((sem, c, e, w, lo, hi))

    def do(q, fn, outs, ins):
        guard(q, outs, ins)
        cnt[q] = cnt.get(q, 0) + 1
        fn().then_inc(T.sem[q], 1)
        note(q, cnt[q], q, outs, ins)

    def ts(o, i, s1, op0, s2=None, op1=None, after=()):
        sc = [s for s in (s1, s2) if isinstance(s, tuple)] + list(after)
        a1 = s1[0] if isinstance(s1, tuple) else s1
        a2 = s2[0] if isinstance(s2, tuple) else s2
        if op1 is None:
            do("V", lambda: g.vector.tensor_scalar(o[0], i[0], a1, None, op0), [o], [i] + sc)
        else:
            do("V", lambda: g.vector.tensor_scalar(o[0], i[0], a1, a2, op0, op1), [o], [i] + sc)

    def tt(o, a, b, op):
        do("V", lambda: g.vector.tensor_tensor(o[0], a[0], b[0], op), [o], [a, b])

    def cp(o, i):
        do("V", lambda: g.vector.tensor_copy(o[0], i[0]), [o], [i])

    def fill(o, c):
        do("V", lambda: g.vector.memset(o[0], c), [o], [])

    def act(o, i, func, bias=0.0, scale=1.0, acc=None):
        cols = [s for s in (bias, scale) if isinstance(s, tuple)]
        b = bias[0] if isinstance(bias, tuple) else bias
        s = scale[0] if isinstance(scale, tuple) else scale
        if acc is None:
            do("S", lambda: g.scalar.activation(o[0], i[0], func, bias=b, scale=s), [o], [i] + cols)
        else:
            do("S", lambda: g.scalar.activation(o[0], i[0], func, bias=b, scale=s, accum_out=acc[0]), [o, acc], [i] + cols)

    def addmult(o, d0, d1):
        do("V", lambda: g.vector.tensor_tensor_scan(o[0], d0[0], d1[0], 0.0, Op.add, Op.mult), [o], [d0, d1])

    def mm(o, l, rh, start=True, stop=True):
        do("T", lambda: g.tensor.matmul(o[0], l[0], rh[0], start, stop), [o], [l, rh])

    def iota(o, pattern, base, cm):
        do("G", lambda: g.iota(o[0], pattern, base, cm, allow_small_or_imprecise_dtypes=True), [o], [])

    def gather(q, o, win, off):
        if q == "V":
            do(q, lambda: g.vector.tensor_copy(o[0], win[0].indirect(off[0])), [o], [win, off])
        else:
            do(q, lambda: g.scalar.activation(o[0], win[0].indirect(off[0]), Act.Copy), [o], [win, off])

    peers, far, sibs = farof(r) + sibof(r), farof(r), sibof(r)
    offm, nearm, full = masks(r)
    offbits = [1 << i for i in range(16) if offm >> i & 1]

    g.sync.dma_start(T.key16[:], T.key[:]).then_inc(T.sem.key, 16)
    note("key", 16, "dkey", [A("key16")], [])
    for i in FIRST:
        lo, hi = PIECES[i]
        g.sync.dma_start(piece(r, i), T.x[:, lo:hi]).then_inc(T.sem["x%d" % i], 16)
        note("x%d" % i, 16, "dx", [A("ld", NT * r + lo, NT * r + hi)], [])

    iota(A("pcol"), [[0, 1]], 0, 1)
    iota(A("iow"), [[1, 160]], 0, 0)
    iota(A("cm16"), [[1, 16]], -15, 0)
    iota(A("jv1"), [[128, 16]], 1, 1)
    iota(A("c33"), [[1, 17], [0, 2]], -16, 0)
    iota(A("io16"), [[0, 16], [1, 16]], 0, 0)
    iota(A("pint"), [[0, 1]], 0, 1)
    w128 = A("iow", 0, 128)
    fill(A("ones"), 1.0)
    fill(A("zz"), 0.0)
    fill(A("ph", 0, 1), 0.0)
    ts(A("z16"), A("zz", 0, 240, p=16), 0.0, Op.mult)
    ts(A("idf"), A("iow", 0, 16, p=16), A("pcol", p=16), Op.is_equal)
    ts(A("z16", 112, 128), A("iow", 0, 16, p=16), A("pcol", p=16), Op.is_equal, after=[A("z16", 112, 128)])
    ts(A("ident"), w128, A("pcol"), Op.is_equal)
    for q in range(4):
        ts(A("pen", 128 * q, 128 * q + 128), w128, A("pcol"), Op.is_le, 0.25, Op.mult)
    ts(A("i16"), w128, 16.0, Op.mult)
    ts(A("abias"), A("pcol"), -16.0, Op.mult, -7.5, Op.add)
    for b in range(16):
        act(A("rowsel", 128 * b, 128 * b + 128), A("ones", 0, 128, p=16), Act.Copy, scale=A("idf", b, b + 1))
    for q in range(2):
        mm(A("kb%d" % q), A("ident"), A("pen"), True, False)
    ts(A("segm"), A("io16"), 0.0, Op.is_gt)
    ts(A("loc", 256, 272), A("ones", 0, 16), 0.0, Op.mult)
    ts(A("tab", 0, 1), A("ones", 0, 1), 0.0, Op.mult)

    def setout(ps):
        for p in ps:
            guard("G", [], [A("ld", NT * r + PIECES[p][0], NT * r + PIECES[p][1])])
            write(piece(r, p), piece(r, p), "tx%d" % (p >= EARLY), helpers(r)[WHO[p]], nearm if p >= EARLY else full)

    setout(FIRST[:EARLY])
    cp(A("kd"), A("key16"))
    for c in range(8):
        mm(A("pt", 0, 16), A("z16", 112 - 16 * c, 240 - 16 * c), A("kd", c, 128, 8), c == 0, c == 7)
    for c in range(8):
        mm(A("pk", 64 + 16 * c, 80 + 16 * c, p=16), A("kd", c, 128, 8), A("z16", 112, 128))
    mm(A("kb2"), A("ident"), A("pen"), True, False)
    cp(A("ktd"), A("pt", 0, 16))
    ts(A("adivi"), A("ktd"), 1.0 / 16, Op.mult, -0.5 + 0.5 / 16, Op.add)
    ts(A("a16"), A("adivi"), 16.0, Op.mult)
    tt(A("u"), A("a16"), A("ktd"), Op.subtract)
    act(A("ktt"), A("pk", 64, 192, p=16), Act.Copy)

    def keyrows(q):
        for b in range(4 * q, 4 * q + 4):
            mm(A("kb%d" % q, 128 * (b % 4), 128 * (b % 4) + 128), A("rowsel", 128 * b, 128 * b + 128), A("ktt"), False, b % 4 == 3)

    def absrow(q):
        act(A("kabs", 512 * q, 512 * q + 512), A("kb%d" % q), Act.Abs, bias=A("abias"))

    def digitrow(q):
        ts(A("oht", 512 * q, 512 * q + 512), A("kabs", 512 * q, 512 * q + 512), 8.0, Op.is_lt)

    def equal(q):
        for b in range(4 * q, 4 * q + 4):
            ts(A("eq", 128 * b, 128 * b + 128), A("kb%d" % q, 128 * (b % 4), 128 * (b % 4) + 128), A("ktd", b, b + 1), Op.is_equal)

    SB = 10
    for b in range(SB):
        act(A("fabs", 16 * b, 16 * b + 16), A("cm16"), Act.Abs, bias=A("u", b, b + 1), scale=-1.0)
    act(A("ohf", 0, 16 * SB), A("fabs", 0, 16 * SB), Act.Relu, bias=A("ones", 0, 1), scale=-1.0)
    for b in range(16):
        ts(A("oha", 128 * b, 128 * b + 128), A("i16"), A("a16", b, b + 1), Op.is_equal)
    for b in range(SB, 16):
        ts(A("ohf", 16 * b, 16 * b + 16), A("cm16"), A("u", b, b + 1), Op.is_equal)
    keyrows(0)
    keyrows(1)
    for b in range(16):
        mm(A("ph", 1 + b, 242 + b, 16), A("oha", 128 * b, 128 * b + 128), A("ohf", 16 * b, 16 * b + 16))
    absrow(0)
    absrow(1)
    addmult(A("loc", 0, 256), A("ph", 0, 256), A("segm"))
    tt(A("hs"), A("loc", 15, 256, 16), A("ph", 16, 257, 16), Op.add)
    guard("G", [], [A("hs")])
    g.remote_dma_fused([RemoteDMATransfer(dst_ids=[dst(d) for d in peers], dma_engine_mask=offm, remote_sem=T.sem.hist, srcs=[T.hs[:]],
                                          dsts=[T.hl[:, 16 * r:16 * r + 16]] * len(peers))], local_sem=T.sem.loc)
    nloc[0] += neng(offm)
    nhist = neng(offm) * len(peers)
    setout(FIRST[EARLY:])
    for d in sibs:
        mine = T.ld[:, NT * r:NT * r + NT]
        write(mine, mine, "dat", T.cores[d], nearm)
    for d in peers:
        note("hist", nhist, "rh", [A("hl", 16 * d, 16 * d + 16)], [])
    mm(A("kb3"), A("ident"), A("pen"), True, False)
    keyrows(2)
    keyrows(3)
    cp(A("hl", 16 * r, 16 * r + 16), A("hs"))
    equal(0)
    digitrow(0)
    equal(1)
    digitrow(1)
    tt(A("ltab"), A("loc", 0, 256), A("loc", 16, 272), Op.subtract)
    absrow(2)
    absrow(3)
    for b in range(16):
        act(A("fx", 33 * b, 33 * b + 33), A("c33", 1, 34), Act.Relu, bias=A("u", b, b + 1), scale=-1.0)
    act(A("m33"), A("fx"), Act.Relu, bias=A("ones", 0, 1), scale=-1.0)
    equal(2)
    digitrow(2)
    equal(3)
    digitrow(3)
    ts(A("lst"), w128, A("pcol"), Op.is_gt)
    ts(A("iowk"), A("iow"), 128.0, Op.mult)
    ts(A("jvn"), A("jv1"), -1.0 / 128, Op.mult)
    acc = lambda b, lo=0, hi=33, step=1: A("pl" if b < 8 else "pt", 33 * (b % 8) + lo, 33 * (b % 8) + hi, step)
    ohb = lambda name, b: A(name, 128 * b, 128 * b + 128)
    for p in ("pl", "pt"):
        mm(A(p, 0, 264), A("ident"), A("zz"), True, False)
    mm(A("pk", 0, 16), A("ident"), A("zz", 0, 16), True, False)
    for b in range(16):
        mm(acc(b, 1, 33, 2), ohb("oht", b), A("ltab", b, 241 + b, 16), False, False)
        mm(acc(b, 32, 33), ohb("eq", b), A("ones", 0, 1), False, False)
    act(A("junk"), A("hl"), Act.Copy, acc=A("rowt"))
    for d in range(N):
        if d < r:
            mm(A("pk", 0, 16), A("ident"), A("hl", 16 * d, 16 * d + 16), False, False)
        else:
            mm(A("pk", 0, 15), A("ident"), A("hl", 16 * d + 1, 16 * d + 16), False, False)
    mm(A("pk", 15, 16), A("lst"), A("rowt"), False, True)
    cp(A("tab", 1, 33, 2), A("pk", 0, 16))
    tt(A("tab", 2, 33, 2), A("pk", 0, 16), A("tab", 1, 33, 2), Op.subtract)
    for b in range(16):
        mm(acc(b), ohb("oht", b), A("tab"), False, b % 8 == 7)
    for h in range(2):
        lo = 264 * h
        addmult(A("scan", lo, lo + 264), A("pl" if h == 0 else "pt", 0, 264), A("m33", lo, lo + 264))
        pos = lambda a, b: A("scan", 33 * a + 32, 33 * (b - 1) + 33, 33)
        ts(A("pdivi", 8 * h, 8 * h + 8), pos(8 * h, 8 * h + 8), 1.0 / 128, Op.mult, -0.5 + 0.5 / 128, Op.add)
        ts(A("pmul", 8 * h, 8 * h + 8), A("pdivi", 8 * h, 8 * h + 8), 128.0, Op.mult)
        for b in range(8 * h, 8 * h + 8):
            ts(ohb("ml", b), w128, A("pmul", b, b + 1), Op.add, pos(b, b + 1), Op.is_equal)
            m = A("mr", 160 * b, 160 * b + 160)
            if b % 8 in (3, 5, 7):
                x = A("mx", 160 * b, 160 * b + 160)
                act(x, A("iowk"), Act.Abs, bias=A("pmul", b, b + 1), scale=-1.0)
                act(m, x, Act.Relu, bias=A("jv1", b, b + 1), scale=A("jvn", b, b + 1))
            else:
                ts(m, A("iowk"), A("pmul", b, b + 1), Op.is_equal, A("jv1", b, b + 1), Op.mult)
            mm(A("kb0", 0, 160), ohb("ml", b), m, b == 0, b == 15)
    ts(A("msk"), A("kb0", 0, 160), 0.0, Op.is_gt, float(NT * r), Op.mult)
    tt(A("mt"), A("kb0", 0, 160), A("msk"), Op.add)
    guard("G", [], [A("mt")])
    nmap = len(far) + neng(nearm) * len(sibs)
    tr = []
    for d in peers:
        m = nearm if d in sibs else offbits[far.index(d) % len(offbits)]
        tr.append(RemoteDMATransfer(dst_ids=[dst(d)], dma_engine_mask=m, remote_sem=T.sem.map,
                                    srcs=[T.mt[:, 16 * d:16 * d + 16]], dsts=[T.lm[:, 16 * r:16 * r + 16]]))
        nloc[0] += neng(m)
        note("map", nmap, "rm", [A("lm", 16 * d, 16 * d + 16)], [])
    g.remote_dma_fused(tr, local_sem=T.sem.loc)
    cp(A("lm", 16 * r, 16 * r + 16), A("mt", 16 * r, 16 * r + 16))
    ts(A("pbit", 0, 1), A("pint"), 15, Op.bitwise_and)
    ts(A("pbit", 1, 2), A("pint"), 4, Op.arith_shift_right)
    cp(A("pdig"), A("pbit"))
    ts(A("wrap"), A("io16", 0, 128), A("pdig", 0, 1), Op.is_equal)
    ts(A("m8"), A("iow", 0, 8), A("pdig", 1, 2), Op.is_equal)
    for c in range(8):
        ts(A("rl", 128 * c, 128 * c + 128), A("wrap"), A("m8", c, c + 1), Op.mult)
    got = neng(nearm) * len(sibs) + sum(neng(m) for q in [r] + sibs for i in range(3) for _, _, _, m in handm(q, i))
    for d in peers:
        note("dat", got, "rd", [A("ld", NT * d, NT * d + NT)], [])
    tt(A("t1"), A("lm", 0, 80), A("lm", 80, 160), Op.add)
    tt(A("t2"), A("t1", 0, 32), A("t1", 32, 64), Op.add)
    tt(A("t3"), A("t2", 0, 16), A("t2", 16, 32), Op.add)
    tt(A("t4"), A("t3"), A("t1", 64, 80), Op.add)
    cp(A("th"), A("t4"))
    tt(A("tl"), A("t4"), A("th"), Op.subtract)
    for c in range(8):
        o = A("kb1", c, 121 + c, 8)
        mm(o, A("rl", 128 * c, 128 * c + 128), A("th"), True, False)
        mm(o, A("rl", 128 * c, 128 * c + 128), A("tl"), False, True)
    ts(A("flist"), A("kb1", 0, 128), -1.0, Op.add)
    for n, (lo, hi) in enumerate(zip(PARTY, PARTY[1:])):
        gather("VS"[n % 2], A("yb", lo, hi), A("ld"), A("flist", lo // 16, hi // 16))
        guard("Y", [], [A("yb", lo, hi)])
        g.sync.dma_start(T.y[:, lo:hi], T.yb[:, lo:hi]).then_inc(T.sem.st, 16)
    for sem, c in ([(q, cnt[q]) for q in "VSTG"] + [("key", 16)] + [("x%d" % i, 16) for i in FIRST]
                   + [("loc", nloc[0]), ("hist", nhist), ("map", nmap), ("dat", got), ("st", 16 * (len(PARTY) - 1))]):
        g.wait_ge(T.sem[sem], c)
